import numpy as np
import ml_dtypes


def mxq(x, axis, fmt="e4m3"):
    dtype, down = {"e4m3": (ml_dtypes.float8_e4m3fn, 7), "e5m2": (ml_dtypes.float8_e5m2, 14)}[fmt]
    v = np.moveaxis(np.asarray(x, np.float32).astype(ml_dtypes.bfloat16).astype(np.float64), axis, -1)
    blocks = v.reshape(v.shape[:-1] + (-1, 32))
    amax = np.abs(blocks).max(-1, keepdims=True)
    byte = np.maximum(np.where(amax > 0, np.frexp(amax)[1] - 1 + 127, 0) - down, 1)
    scale = np.exp2(byte - 127.0)
    codes = (blocks / scale).astype(np.float32).astype(dtype).astype(np.float64)
    return np.moveaxis((codes * scale).reshape(v.shape), -1, axis)


WIDE = False


def mx_kscale(k):
    if not WIDE:
        return np.ones(k)
    levels = np.array([10, -10, 5, -5, 0])
    if k % 512:
        return np.exp2(np.random.permutation(np.resize(levels, k // 32))).repeat(32)
    a = np.empty((k // 512, 16))
    for p in range(k // 512):
        a[p, :8] = np.random.permutation(np.resize(levels, 8))
        for g in range(8):
            far = levels[np.abs(levels - a[p, g]) >= 10]
            a[p, g + 8] = far[np.random.randint(len(far))]
    return np.exp2(a.ravel()).repeat(32)


def f64(x):
    return np.asarray(x).astype(np.float64)


def striped(idx):
    return np.tile(idx.reshape(-1, 16).T, (8, 1)).astype(np.uint16)


def unstriped(offs):
    return offs[:16].T.reshape(-1).astype(np.int64)


def pack_weight(w):
    k, n = w.shape
    w = f64(np.asarray(w, np.float32).astype(ml_dtypes.bfloat16)).reshape(k // 32, 32, n)
    amax = np.abs(w).max(1)
    byte = np.clip(np.where(amax > 0, np.frexp(amax)[1] - 1 + 127 - 7, 1), 1, 254)
    scaled = (w * np.exp2(127.0 - byte)[:, None, :]).reshape(k, n).astype(np.float32)
    words = np.ascontiguousarray(scaled.reshape(k // 512, 128, 4, n).transpose(0, 1, 3, 2)).astype(ml_dtypes.float8_e4m3fn).view(np.uint8)
    return words, np.ascontiguousarray(byte.astype(np.uint8).reshape(k // 512, 16, n))


def unpack_weight(words, scales):
    g, p, n, _ = words.shape
    vals = np.ascontiguousarray(words).view(ml_dtypes.float8_e4m3fn).astype(np.float64) * np.repeat(np.exp2(scales.astype(np.float64) - 127.0), 8, axis=1)[..., None]
    return vals.transpose(0, 1, 3, 2).reshape(g * 512, n)


K, T, E, C, N = 2048, 512, 8, 128, 128


def by_expert(wq, xq):
    return np.concatenate([wq[e].T @ xq[:, e * C:(e + 1) * C] for e in range(E)], axis=1)


def setup_inputs():
    n = np.random.standard_normal
    s = mx_kscale(K)[:, None]
    first = np.random.permutation(np.repeat(np.arange(E), T // E))
    second = (first + 1 + np.random.permutation(np.repeat(np.arange(E - 1), -(-T // (E - 1)))[:T])) % E
    while np.bincount(second, minlength=E).max() != T // E:
        load = np.bincount(second, minlength=E); hi, lo = int(load.argmax()), int(load.argmin())
        t = np.flatnonzero((second == hi) & (first != lo))[0]; second[t] = lo
    slot_token = np.empty(E * C, np.int64); pos = np.empty((2, T), np.int64); fill = np.zeros(E, np.int64)
    place = np.stack([np.random.permutation(C) for _ in range(E)])
    for r, deal in enumerate((first, second)):
        for t in np.random.permutation(T):
            e = deal[t]; j = e * C + place[e, fill[e]]; fill[e] += 1; slot_token[j] = t; pos[r, t] = j
    g = np.random.uniform(0.2, 0.8, T)
    packed = [pack_weight(m) for m in n((E, K, N)) / np.sqrt(K) / s[None]]
    return {
        "xT": (n((K, T)) * s).astype(np.float32),
        "w_words": np.stack([m[0] for m in packed]),
        "w_scales": np.stack([m[1] for m in packed]),
        "gate": np.stack([np.tile(g, (N, 1)), np.tile(1.0 - g, (N, 1))]).astype(np.float32),
        "offs": striped(slot_token),
        "pos1": striped(pos[0]),
        "pos2": striped(pos[1]),
    }


def reference(xT, w_words, w_scales, gate, offs, pos1, pos2):
    idx = unstriped(offs)
    xq = mxq(f64(xT)[:, idx], 0, "e4m3")
    w = np.stack([unpack_weight(w_words[e], w_scales[e]) for e in range(E)])
    y = by_expert(w, xq)
    return f64(gate[0]) * y[:, unstriped(pos1)] + f64(gate[1]) * y[:, unstriped(pos2)]

@@ -1,0 +1,111 @@
+from contextlib import ExitStack
+
+import concourse.mybir as mybir
+
+K, T, E, C, N = 2048, 512, 8, 128, 128
+FLOPS = 2 * K * N * E * C
+
+F32 = mybir.dt.float32
+BF16 = mybir.dt.bfloat16
+I32 = mybir.dt.int32
+U32 = mybir.dt.uint32
+U16 = mybir.dt.uint16
+U8 = mybir.dt.uint8
+FP8X4 = mybir.dt.float8_e4m3fn_x4
+MULT = mybir.AluOpType.mult
+ADD = mybir.AluOpType.add
+
+P = 128
+PACK = 4
+PASSES = K // (P * PACK)
+SLOTS = E * C
+CUT = 256
+CUTS = SLOTS // CUT
+EXPERTS_A_CUT = CUT // C
+
+
+def tile_routed_moe_kernel(tc, xT, w_words, w_scales, gate, offs, pos1, pos2, out):
+    nc = tc.nc
+    with ExitStack() as ctx:
+        lists = ctx.enter_context(tc.tile_pool(name="lists", bufs=1))
+        keep = ctx.enter_context(tc.tile_pool(name="keep", bufs=1))
+        ring = ctx.enter_context(tc.tile_pool(name="ring", bufs=3))
+        codes = ctx.enter_context(tc.tile_pool(name="codes", bufs=4))
+        psum = ctx.enter_context(tc.psum_pool(name="psum", bufs=1))
+
+        offs_t = lists.tile([P, SLOTS // 16], U16, name="offs_t")
+        pos1_t = lists.tile([P, T // 16], U16, name="pos1_t")
+        pos2_t = lists.tile([P, T // 16], U16, name="pos2_t")
+        nc.sync.dma_start(offs_t[:], offs)
+
+        w_scale_t = keep.tile([P, E * PASSES, N], U8, name="w_scale_t", align_bytes=64)
+        nc.vector.memset(w_scale_t[:].rearrange("p b n -> p (b n)").bitcast(I32), 0)
+
+        x_planes = xT.rearrange("(a p t) n -> a p t n", p=P, t=PACK)
+        planes = [[keep.tile([P, T], F32, name="plane%d_%d" % (a, t)) for t in range(PACK)] for a in range(PASSES)]
+        w_code_t = [keep.tile([P, E, N], I32, name="w_code%d" % a, align_bytes=64) for a in range(PASSES)]
+
+        for a in range(PASSES):
+            for t in range(PACK):
+                nc.sync.dma_start(planes[a][t][:], x_planes[a, :, t, :])
+            if a == 0:
+                for q in range(4):
+                    nc.sync.dma_start(
+                        w_scale_t[32 * q : 32 * q + 4, :, :].bitcast(I32),
+                        w_scales[:, :, 4 * q : 4 * q + 4, :].rearrange("e a r n -> r (e a) n").bitcast(I32),
+                    )
+            nc.sync.dma_start(w_code_t[a][:], w_words[:, a].rearrange("e p n r -> p e (n r)").bitcast(I32))
+        nc.sync.dma_start(pos1_t[:], pos1)
+        nc.sync.dma_start(pos2_t[:], pos2)
+        gate_t = [keep.tile([P, T], F32, name="gate%d" % r) for r in range(2)]
+        for r in range(2):
+            nc.sync.dma_start(gate_t[r][:], gate[r])
+
+        acc = [psum.tile([P, C], F32, name="acc%d" % e) for e in range(E)]
+        y = keep.tile([P, SLOTS], F32, name="y")
+
+        def gather(a, s):
+            g4 = ring.tile([P, PACK, CUT], F32, name="g4")
+            for t in range(PACK):
+                nc.vector.tensor_copy(g4[:, t, :], planes[a][t][:].indirect(offs_t[:, s * (CUT // 16) : (s + 1) * (CUT // 16)]))
+            return g4
+
+        def interleave(g4):
+            grouped = ring.tile([P, CUT, PACK], BF16, name="grouped", align_bytes=64)
+            nc.scalar.copy(grouped[:], g4[:].rearrange("p t n -> p n t"))
+            return grouped
+
+        def quantise_and_multiply(a, s, grouped):
+            x_code = codes.tile([P, CUT], U32, name="x_code", align_bytes=64)
+            x_scale = codes.tile([P, CUT], U8, name="x_scale", align_bytes=64)
+            nc.vector.quantize_mx(out=x_code[:].bitcast(FP8X4), scales=x_scale[:], in_=grouped[:].rearrange("p n t -> p (n t)"))
+            for i in range(EXPERTS_A_CUT):
+                e = s * EXPERTS_A_CUT + i
+                nc.tensor.matmul_mx(
+                    out=acc[e][:],
+                    lhsT=w_code_t[a][:, e, :].bitcast(FP8X4),
+                    lhsT_scale=w_scale_t[:, e * PASSES + a, :],
+                    rhs=x_code[:, i * C : (i + 1) * C].bitcast(FP8X4),
+                    rhs_scale=x_scale[:, i * C : (i + 1) * C],
+                    start=(a == 0),
+                    stop=(a == PASSES - 1),
+                )
+                if a == PASSES - 1:
+                    nc.scalar.copy(y[:, e * C : (e + 1) * C], acc[e][:])
+
+        units = [(a, s) for a in range(PASSES) for s in range(CUTS)]
+        waiting = None
+        for a, s in units:
+            g4 = gather(a, s)
+            if waiting is not None:
+                quantise_and_multiply(*waiting)
+            waiting = (a, s, interleave(g4))
+        quantise_and_multiply(*waiting)
+
+        first = keep.tile([P, T], F32, name="first")
+        second = keep.tile([P, T], F32, name="second")
+        result = keep.tile([P, T], F32, name="result")
+        nc.vector.tensor_tensor(first[:], y[:].indirect(pos1_t[:]), gate_t[0][:], MULT)
+        nc.vector.tensor_tensor(second[:], y[:].indirect(pos2_t[:]), gate_t[1][:], MULT)
+        nc.vector.tensor_tensor(result[:], first[:], second[:], ADD)
+        nc.sync.dma_start(out, result[:])

@@ -14,14 +14,27 @@ U8 = mybir.dt.uint8
 FP8X4 = mybir.dt.float8_e4m3fn_x4
 MULT = mybir.AluOpType.mult
 ADD = mybir.AluOpType.add
+COPY = mybir.ActivationFunctionType.Copy
 
 P = 128
 PACK = 4
 PASSES = K // (P * PACK)
 SLOTS = E * C
-CUT = 256
-CUTS = SLOTS // CUT
-EXPERTS_A_CUT = CUT // C
+PAIR = 2 * C
+
+CUTS = ((0, 0, 384), (0, 384, 768), (0, 768, 1024), (1, 0, 384), (1, 384, 768), (1, 768, 1024), (2, 768, 1024))
+GROUPS = (
+    ((0, 0, 256), ()),
+    ((0, 256, 768), ()),
+    ((0, 768, 1024), ((3, 0),)),
+    ((1, 0, 256), ((3, 1),)),
+    ((1, 256, 768), ((3, 2), (3, 3))),
+    ((1, 768, 1024), ((2, 0),)),
+    ((2, 768, 1024), ((2, 1),)),
+    (None, ((2, 2),)),
+)
+S_PASSES = (3, 2)
+Y_COPY_ON_SCALAR = (0, 1, 4)
 
 
 def tile_routed_moe_kernel(tc, xT, w_words, w_scales, gate, offs, pos1, pos2, out):
@@ -30,7 +43,6 @@ def tile_routed_moe_kernel(tc, xT, w_words, w_scales, gate, offs, pos1, pos2, ou
         lists = ctx.enter_context(tc.tile_pool(name="lists", bufs=1))
         keep = ctx.enter_context(tc.tile_pool(name="keep", bufs=1))
         ring = ctx.enter_context(tc.tile_pool(name="ring", bufs=3))
-        codes = ctx.enter_context(tc.tile_pool(name="codes", bufs=4))
         psum = ctx.enter_context(tc.psum_pool(name="psum", bufs=1))
 
         offs_t = lists.tile([P, SLOTS // 16], U16, name="offs_t")
@@ -45,16 +57,25 @@ def tile_routed_moe_kernel(tc, xT, w_words, w_scales, gate, offs, pos1, pos2, ou
         planes = [[keep.tile([P, T], F32, name="plane%d_%d" % (a, t)) for t in range(PACK)] for a in range(PASSES)]
         w_code_t = [keep.tile([P, E, N], I32, name="w_code%d" % a, align_bytes=64) for a in range(PASSES)]
 
-        for a in range(PASSES):
-            for t in range(PACK):
-                nc.sync.dma_start(planes[a][t][:], x_planes[a, :, t, :])
-            if a == 0:
-                for q in range(4):
-                    nc.sync.dma_start(
-                        w_scale_t[32 * q : 32 * q + 4, :, :].bitcast(I32),
-                        w_scales[:, :, 4 * q : 4 * q + 4, :].rearrange("e a r n -> r (e a) n").bitcast(I32),
-                    )
+        def load_plane(a, t):
+            nc.sync.dma_start(planes[a][t][:], x_planes[a, :, t, :])
+
+        def load_codes(a):
             nc.sync.dma_start(w_code_t[a][:], w_words[:, a].rearrange("e p n r -> p e (n r)").bitcast(I32))
+
+        for a, t in ((0, 0), (0, 1), (0, 2), (3, 0), (0, 3), (3, 1), (3, 2), (3, 3)):
+            load_plane(a, t)
+        for q in range(4):
+            nc.sync.dma_start(
+                w_scale_t[32 * q : 32 * q + 4, :, :].bitcast(I32),
+                w_scales[:, :, 4 * q : 4 * q + 4, :].rearrange("e a r n -> r (e a) n").bitcast(I32),
+            )
+        load_codes(0)
+        load_codes(3)
+        for a in (1, 2):
+            for t in range(PACK):
+                load_plane(a, t)
+            load_codes(a)
         nc.sync.dma_start(pos1_t[:], pos1)
         nc.sync.dma_start(pos2_t[:], pos2)
         gate_t = [keep.tile([P, T], F32, name="gate%d" % r) for r in range(2)]
@@ -63,44 +84,94 @@ def tile_routed_moe_kernel(tc, xT, w_words, w_scales, gate, offs, pos1, pos2, ou
 
         acc = [psum.tile([P, C], F32, name="acc%d" % e) for e in range(E)]
         y = keep.tile([P, SLOTS], F32, name="y")
+        passes_done = [0] * E
 
-        def gather(a, s):
-            g4 = ring.tile([P, PACK, CUT], F32, name="g4")
+        def v_width(g):
+            return 0 if GROUPS[g][0] is None else GROUPS[g][0][2] - GROUPS[g][0][1]
+
+        widths = [v_width(g) + PAIR * len(GROUPS[g][1]) for g in range(len(GROUPS))]
+        grouped = [keep.tile([P, widths[g] * PACK], BF16, name="grouped%d" % g, align_bytes=64) for g in range(len(GROUPS))]
+        x_code = [keep.tile([P, widths[g]], U32, name="x_code%d" % g, align_bytes=64) for g in range(len(GROUPS))]
+        x_scale = [keep.tile([P, widths[g]], U8, name="x_scale%d" % g, align_bytes=64) for g in range(len(GROUPS))]
+
+        for a in S_PASSES:
+            rounded = keep.tile([P, PACK, T], BF16, name="rounded%d" % a)
             for t in range(PACK):
-                nc.vector.tensor_copy(g4[:, t, :], planes[a][t][:].indirect(offs_t[:, s * (CUT // 16) : (s + 1) * (CUT // 16)]))
-            return g4
+                nc.scalar.copy(rounded[:, t, :], planes[a][t][:])
+            for g in range(len(GROUPS)):
+                for i, (pair_pass, pair) in enumerate(GROUPS[g][1]):
+                    if pair_pass != a:
+                        continue
+                    view = grouped[g][:].rearrange("p (n t) -> p n t", t=PACK)
+                    for h in range(2):
+                        e = 2 * pair + h
+                        col = v_width(g) + i * PAIR + h * C
+                        for t in range(PACK):
+                            nc.scalar.activation(
+                                view[:, col : col + C, t],
+                                rounded[:, t, :].indirect(offs_t[:, e * (C // 16) : (e + 1) * (C // 16)]),
+                                COPY,
+                            )
 
-        def interleave(g4):
-            grouped = ring.tile([P, CUT, PACK], BF16, name="grouped", align_bytes=64)
-            nc.scalar.copy(grouped[:], g4[:].rearrange("p t n -> p n t"))
-            return grouped
-
-        def quantise_and_multiply(a, s, grouped):
-            x_code = codes.tile([P, CUT], U32, name="x_code", align_bytes=64)
-            x_scale = codes.tile([P, CUT], U8, name="x_scale", align_bytes=64)
-            nc.vector.quantize_mx(out=x_code[:].bitcast(FP8X4), scales=x_scale[:], in_=grouped[:].rearrange("p n t -> p (n t)"))
-            for i in range(EXPERTS_A_CUT):
-                e = s * EXPERTS_A_CUT + i
-                nc.tensor.matmul_mx(
-                    out=acc[e][:],
-                    lhsT=w_code_t[a][:, e, :].bitcast(FP8X4),
-                    lhsT_scale=w_scale_t[:, e * PASSES + a, :],
-                    rhs=x_code[:, i * C : (i + 1) * C].bitcast(FP8X4),
-                    rhs_scale=x_scale[:, i * C : (i + 1) * C],
-                    start=(a == 0),
-                    stop=(a == PASSES - 1),
-                )
-                if a == PASSES - 1:
+        def multiply(g, a, e, col):
+            nc.tensor.matmul_mx(
+                out=acc[e][:],
+                lhsT=w_code_t[a][:, e, :].bitcast(FP8X4),
+                lhsT_scale=w_scale_t[:, e * PASSES + a, :],
+                rhs=x_code[g][:, col : col + C].bitcast(FP8X4),
+                rhs_scale=x_scale[g][:, col : col + C],
+                start=(passes_done[e] == 0),
+                stop=(passes_done[e] == PASSES - 1),
+            )
+            passes_done[e] += 1
+            if passes_done[e] == PASSES:
+                if e in Y_COPY_ON_SCALAR:
                     nc.scalar.copy(y[:, e * C : (e + 1) * C], acc[e][:])
+                else:
+                    nc.vector.tensor_copy(y[:, e * C : (e + 1) * C], acc[e][:])
 
-        units = [(a, s) for a in range(PASSES) for s in range(CUTS)]
-        waiting = None
-        for a, s in units:
-            g4 = gather(a, s)
-            if waiting is not None:
-                quantise_and_multiply(*waiting)
-            waiting = (a, s, interleave(g4))
-        quantise_and_multiply(*waiting)
+        def quantise(g):
+            nc.vector.quantize_mx(out=x_code[g][:].bitcast(FP8X4), scales=x_scale[g][:], in_=grouped[g][:])
+            if GROUPS[g][0] is not None:
+                a, lo, hi = GROUPS[g][0]
+                for e in range(lo // C, hi // C):
+                    multiply(g, a, e, e * C - lo)
+            for i, (a, pair) in enumerate(GROUPS[g][1]):
+                for h in range(2):
+                    multiply(g, a, 2 * pair + h, v_width(g) + i * PAIR + h * C)
+
+        g4_of = {}
+
+        def gather(k):
+            a, lo, hi = CUTS[k]
+            g4 = ring.tile([P, PACK, hi - lo], F32, name="g4")
+            for t in range(PACK):
+                nc.vector.tensor_copy(g4[:, t, :], planes[a][t][:].indirect(offs_t[:, lo // 16 : hi // 16]))
+            g4_of[k] = g4
+
+        def interleave(k):
+            a, lo, hi = CUTS[k]
+            for g in range(len(GROUPS)):
+                if GROUPS[g][0] is None or GROUPS[g][0][0] != a:
+                    continue
+                b0, b1 = max(lo, GROUPS[g][0][1]), min(hi, GROUPS[g][0][2])
+                if b0 >= b1:
+                    continue
+                g_lo = GROUPS[g][0][1]
+                nc.vector.tensor_copy(
+                    grouped[g][:, (b0 - g_lo) * PACK : (b1 - g_lo) * PACK].rearrange("p (n t) -> p n t", t=PACK),
+                    g4_of[k][:, :, b0 - lo : b1 - lo].rearrange("p t n -> p n t"),
+                )
+
+        n_cuts = len(CUTS)
+        for k in range(n_cuts + 2):
+            if k < n_cuts:
+                gather(k)
+            if 1 <= k <= n_cuts:
+                interleave(k - 1)
+            if k >= 2:
+                quantise(k - 2)
+        quantise(len(GROUPS) - 1)
 
         first = keep.tile([P, T], F32, name="first")
         second = keep.tile([P, T], F32, name="second")

@@ -20,21 +20,19 @@ P = 128
 PACK = 4
 PASSES = K // (P * PACK)
 SLOTS = E * C
-PAIR = 2 * C
 
-CUTS = ((0, 0, 384), (0, 384, 768), (0, 768, 1024), (1, 0, 384), (1, 384, 768), (1, 768, 1024), (2, 768, 1024))
+PASS_PAIRS = ((0, 3), (1, 2))
+CUTS = ((0, 0, 512), (0, 512, 1024), (1, 0, 512), (1, 512, 1024))
 GROUPS = (
-    ((0, 0, 256), ()),
-    ((0, 256, 768), ()),
-    ((0, 768, 1024), ((3, 0),)),
-    ((1, 0, 256), ((3, 1),)),
-    ((1, 256, 768), ((3, 2), (3, 3))),
-    ((1, 768, 1024), ((2, 0),)),
-    ((2, 768, 1024), ((2, 1),)),
-    (None, ((2, 2),)),
+    ((0, 0, 512), ()),
+    ((0, 512, 1024), ((3, 0, 4),)),
+    ((1, 0, 512), ((3, 4, 4),)),
+    ((1, 512, 1024), ((2, 0, 4),)),
+    (None, ((2, 4, 2),)),
+    (None, ((2, 6, 1),)),
+    (None, ((2, 7, 1),)),
 )
-S_PASSES = (3, 2)
-Y_COPY_ON_SCALAR = (0, 1, 4)
+Y_COPY_ON_SCALAR = (6,)
 
 
 def tile_routed_moe_kernel(tc, xT, w_words, w_scales, gate, offs, pos1, pos2, out):
@@ -54,28 +52,28 @@ def tile_routed_moe_kernel(tc, xT, w_words, w_scales, gate, offs, pos1, pos2, ou
         nc.vector.memset(w_scale_t[:].rearrange("p b n -> p (b n)").bitcast(I32), 0)
 
         x_planes = xT.rearrange("(a p t) n -> a p t n", p=P, t=PACK)
-        planes = [[keep.tile([P, T], F32, name="plane%d_%d" % (a, t)) for t in range(PACK)] for a in range(PASSES)]
+        two_planes = [[keep.tile([P, 2, T], F32, name="planes%d_%d" % (i, t)) for t in range(PACK)] for i in range(len(PASS_PAIRS))]
         w_code_t = [keep.tile([P, E, N], I32, name="w_code%d" % a, align_bytes=64) for a in range(PASSES)]
 
-        def load_plane(a, t):
-            nc.sync.dma_start(planes[a][t][:], x_planes[a, :, t, :])
+        def load_planes(i):
+            for t in range(PACK):
+                nc.sync.dma_start(two_planes[i][t][:, 1, :], x_planes[PASS_PAIRS[i][1], :, t, :])
+                nc.sync.dma_start(two_planes[i][t][:, 0, :], x_planes[PASS_PAIRS[i][0], :, t, :])
 
         def load_codes(a):
             nc.sync.dma_start(w_code_t[a][:], w_words[:, a].rearrange("e p n r -> p e (n r)").bitcast(I32))
 
-        for a, t in ((0, 0), (0, 1), (0, 2), (3, 0), (0, 3), (3, 1), (3, 2), (3, 3)):
-            load_plane(a, t)
+        load_planes(0)
         for q in range(4):
             nc.sync.dma_start(
                 w_scale_t[32 * q : 32 * q + 4, :, :].bitcast(I32),
                 w_scales[:, :, 4 * q : 4 * q + 4, :].rearrange("e a r n -> r (e a) n").bitcast(I32),
             )
         load_codes(0)
+        load_planes(1)
         load_codes(3)
-        for a in (1, 2):
-            for t in range(PACK):
-                load_plane(a, t)
-            load_codes(a)
+        load_codes(1)
+        load_codes(2)
         nc.sync.dma_start(pos1_t[:], pos1)
         nc.sync.dma_start(pos2_t[:], pos2)
         gate_t = [keep.tile([P, T], F32, name="gate%d" % r) for r in range(2)]
@@ -89,29 +87,34 @@ def tile_routed_moe_kernel(tc, xT, w_words, w_scales, gate, offs, pos1, pos2, ou
         def v_width(g):
             return 0 if GROUPS[g][0] is None else GROUPS[g][0][2] - GROUPS[g][0][1]
 
-        widths = [v_width(g) + PAIR * len(GROUPS[g][1]) for g in range(len(GROUPS))]
-        grouped = [keep.tile([P, widths[g] * PACK], BF16, name="grouped%d" % g, align_bytes=64) for g in range(len(GROUPS))]
-        x_code = [keep.tile([P, widths[g]], U32, name="x_code%d" % g, align_bytes=64) for g in range(len(GROUPS))]
-        x_scale = [keep.tile([P, widths[g]], U8, name="x_scale%d" % g, align_bytes=64) for g in range(len(GROUPS))]
+        n_groups = len(GROUPS)
+        widths = [v_width(g) + C * sum(run[2] for run in GROUPS[g][1]) for g in range(n_groups)]
+        grouped = [keep.tile([P, widths[g] * PACK], BF16, name="grouped%d" % g, align_bytes=64) for g in range(n_groups)]
+        x_code = [keep.tile([P, widths[g]], U32, name="x_code%d" % g, align_bytes=64) for g in range(n_groups)]
+        x_scale = [keep.tile([P, widths[g]], U8, name="x_scale%d" % g, align_bytes=64) for g in range(n_groups)]
 
-        for a in S_PASSES:
-            rounded = keep.tile([P, PACK, T], BF16, name="rounded%d" % a)
+        scalar_share = []
+        for g in range(n_groups):
+            col = v_width(g)
+            for a, e0, count in GROUPS[g][1]:
+                for e in range(e0, e0 + count):
+                    scalar_share.append((g, a, e, col))
+                    col += C
+
+        for i in range(len(PASS_PAIRS)):
+            s_pass = PASS_PAIRS[i][1]
+            rounded = keep.tile([P, PACK, T], BF16, name="rounded%d" % s_pass)
             for t in range(PACK):
-                nc.scalar.copy(rounded[:, t, :], planes[a][t][:])
-            for g in range(len(GROUPS)):
-                for i, (pair_pass, pair) in enumerate(GROUPS[g][1]):
-                    if pair_pass != a:
-                        continue
+                nc.vector.tensor_copy(rounded[:, t, :], two_planes[i][t][:, 1, :])
+            for g, a, e, col in scalar_share:
+                if a == s_pass:
                     view = grouped[g][:].rearrange("p (n t) -> p n t", t=PACK)
-                    for h in range(2):
-                        e = 2 * pair + h
-                        col = v_width(g) + i * PAIR + h * C
-                        for t in range(PACK):
-                            nc.scalar.activation(
-                                view[:, col : col + C, t],
-                                rounded[:, t, :].indirect(offs_t[:, e * (C // 16) : (e + 1) * (C // 16)]),
-                                COPY,
-                            )
+                    for t in range(PACK):
+                        nc.scalar.activation(
+                            view[:, col : col + C, t],
+                            rounded[:, t, :].indirect(offs_t[:, e * (C // 16) : (e + 1) * (C // 16)]),
+                            COPY,
+                        )
 
         def multiply(g, a, e, col):
             nc.tensor.matmul_mx(
@@ -136,32 +139,25 @@ def tile_routed_moe_kernel(tc, xT, w_words, w_scales, gate, offs, pos1, pos2, ou
                 a, lo, hi = GROUPS[g][0]
                 for e in range(lo // C, hi // C):
                     multiply(g, a, e, e * C - lo)
-            for i, (a, pair) in enumerate(GROUPS[g][1]):
-                for h in range(2):
-                    multiply(g, a, 2 * pair + h, v_width(g) + i * PAIR + h * C)
+            for g2, a, e, col in scalar_share:
+                if g2 == g:
+                    multiply(g, a, e, col)
 
         g4_of = {}
 
         def gather(k):
             a, lo, hi = CUTS[k]
+            i = [pair[0] for pair in PASS_PAIRS].index(a)
             g4 = ring.tile([P, PACK, hi - lo], F32, name="g4")
             for t in range(PACK):
-                nc.vector.tensor_copy(g4[:, t, :], planes[a][t][:].indirect(offs_t[:, lo // 16 : hi // 16]))
+                nc.vector.tensor_copy(g4[:, t, :], two_planes[i][t][:].rearrange("p h n -> p (h n)").indirect(offs_t[:, lo // 16 : hi // 16]))
             g4_of[k] = g4
 
         def interleave(k):
-            a, lo, hi = CUTS[k]
-            for g in range(len(GROUPS)):
-                if GROUPS[g][0] is None or GROUPS[g][0][0] != a:
-                    continue
-                b0, b1 = max(lo, GROUPS[g][0][1]), min(hi, GROUPS[g][0][2])
-                if b0 >= b1:
-                    continue
-                g_lo = GROUPS[g][0][1]
-                nc.vector.tensor_copy(
-                    grouped[g][:, (b0 - g_lo) * PACK : (b1 - g_lo) * PACK].rearrange("p (n t) -> p n t", t=PACK),
-                    g4_of[k][:, :, b0 - lo : b1 - lo].rearrange("p t n -> p n t"),
-                )
+            nc.vector.tensor_copy(
+                grouped[k][:, 0 : v_width(k) * PACK].rearrange("p (n t) -> p n t", t=PACK),
+                g4_of[k][:].rearrange("p t n -> p n t"),
+            )
 
         n_cuts = len(CUTS)
         for k in range(n_cuts + 2):
@@ -171,7 +167,8 @@ def tile_routed_moe_kernel(tc, xT, w_words, w_scales, gate, offs, pos1, pos2, ou
                 interleave(k - 1)
             if k >= 2:
                 quantise(k - 2)
-        quantise(len(GROUPS) - 1)
+        for g in range(n_cuts, n_groups):
+            quantise(g)
 
         first = keep.tile([P, T], F32, name="first")
         second = keep.tile([P, T], F32, name="second")

@@ -22,17 +22,19 @@ PASSES = K // (P * PACK)
 SLOTS = E * C
 
 PASS_PAIRS = ((0, 3), (1, 2))
-CUTS = ((0, 0, 512), (0, 512, 1024), (1, 0, 512), (1, 512, 1024))
+CUTS = ((0, 0, 512), (0, 512, 1024), (1, 768, 1024))
+S_PASSES = (3, 2, 1)
 GROUPS = (
     ((0, 0, 512), ()),
     ((0, 512, 1024), ((3, 0, 4),)),
-    ((1, 0, 512), ((3, 4, 4),)),
-    ((1, 512, 1024), ((2, 0, 4),)),
-    (None, ((2, 4, 2),)),
-    (None, ((2, 6, 1),)),
-    (None, ((2, 7, 1),)),
+    (None, ((3, 4, 4), (2, 0, 4))),
+    ((1, 768, 1024), ()),
+    (None, ((2, 4, 4),)),
+    (None, ((1, 0, 4),)),
+    (None, ((1, 4, 1),)),
+    (None, ((1, 5, 1),)),
 )
-Y_COPY_ON_SCALAR = (6,)
+Y_COPY_ON_VECTOR = (5, 6, 7)
 
 
 def tile_routed_moe_kernel(tc, xT, w_words, w_scales, gate, offs, pos1, pos2, out):
@@ -40,7 +42,6 @@ def tile_routed_moe_kernel(tc, xT, w_words, w_scales, gate, offs, pos1, pos2, ou
     with ExitStack() as ctx:
         lists = ctx.enter_context(tc.tile_pool(name="lists", bufs=1))
         keep = ctx.enter_context(tc.tile_pool(name="keep", bufs=1))
-        ring = ctx.enter_context(tc.tile_pool(name="ring", bufs=3))
         psum = ctx.enter_context(tc.psum_pool(name="psum", bufs=1))
 
         offs_t = lists.tile([P, SLOTS // 16], U16, name="offs_t")
@@ -54,26 +55,22 @@ def tile_routed_moe_kernel(tc, xT, w_words, w_scales, gate, offs, pos1, pos2, ou
         x_planes = xT.rearrange("(a p t) n -> a p t n", p=P, t=PACK)
         two_planes = [[keep.tile([P, 2, T], F32, name="planes%d_%d" % (i, t)) for t in range(PACK)] for i in range(len(PASS_PAIRS))]
         w_code_t = [keep.tile([P, E, N], I32, name="w_code%d" % a, align_bytes=64) for a in range(PASSES)]
+        where = {}
+        for i in range(len(PASS_PAIRS)):
+            for h in range(2):
+                where[PASS_PAIRS[i][h]] = (i, h)
 
-        def load_planes(i):
+        for i in range(len(PASS_PAIRS)):
             for t in range(PACK):
-                nc.sync.dma_start(two_planes[i][t][:, 1, :], x_planes[PASS_PAIRS[i][1], :, t, :])
-                nc.sync.dma_start(two_planes[i][t][:, 0, :], x_planes[PASS_PAIRS[i][0], :, t, :])
-
-        def load_codes(a):
-            nc.sync.dma_start(w_code_t[a][:], w_words[:, a].rearrange("e p n r -> p e (n r)").bitcast(I32))
-
-        load_planes(0)
+                for h in (1, 0):
+                    nc.sync.dma_start(two_planes[i][t][:, h, :], x_planes[PASS_PAIRS[i][h], :, t, :])
         for q in range(4):
             nc.sync.dma_start(
                 w_scale_t[32 * q : 32 * q + 4, :, :].bitcast(I32),
                 w_scales[:, :, 4 * q : 4 * q + 4, :].rearrange("e a r n -> r (e a) n").bitcast(I32),
             )
-        load_codes(0)
-        load_planes(1)
-        load_codes(3)
-        load_codes(1)
-        load_codes(2)
+        for a in (0, 3, 2, 1):
+            nc.sync.dma_start(w_code_t[a][:], w_words[:, a].rearrange("e p n r -> p e (n r)").bitcast(I32))
         nc.sync.dma_start(pos1_t[:], pos1)
         nc.sync.dma_start(pos2_t[:], pos2)
         gate_t = [keep.tile([P, T], F32, name="gate%d" % r) for r in range(2)]
@@ -93,28 +90,36 @@ def tile_routed_moe_kernel(tc, xT, w_words, w_scales, gate, offs, pos1, pos2, ou
         x_code = [keep.tile([P, widths[g]], U32, name="x_code%d" % g, align_bytes=64) for g in range(n_groups)]
         x_scale = [keep.tile([P, widths[g]], U8, name="x_scale%d" % g, align_bytes=64) for g in range(n_groups)]
 
-        scalar_share = []
+        runs = []
         for g in range(n_groups):
             col = v_width(g)
             for a, e0, count in GROUPS[g][1]:
-                for e in range(e0, e0 + count):
-                    scalar_share.append((g, a, e, col))
-                    col += C
+                pairs = keep.tile([P, 2, count * C, 2], BF16, name="pairs%d_%d" % (a, e0))
+                runs.append((g, a, e0, count, col, pairs))
+                col += count * C
 
-        for i in range(len(PASS_PAIRS)):
-            s_pass = PASS_PAIRS[i][1]
+        for s_pass in S_PASSES:
+            i, half = where[s_pass]
             rounded = keep.tile([P, PACK, T], BF16, name="rounded%d" % s_pass)
             for t in range(PACK):
-                nc.vector.tensor_copy(rounded[:, t, :], two_planes[i][t][:, 1, :])
-            for g, a, e, col in scalar_share:
+                nc.vector.tensor_copy(rounded[:, t, :], two_planes[i][t][:, half, :])
+            for g, a, e0, count, col, pairs in runs:
                 if a == s_pass:
-                    view = grouped[g][:].rearrange("p (n t) -> p n t", t=PACK)
-                    for t in range(PACK):
-                        nc.scalar.activation(
-                            view[:, col : col + C, t],
-                            rounded[:, t, :].indirect(offs_t[:, e * (C // 16) : (e + 1) * (C // 16)]),
-                            COPY,
-                        )
+                    for j in range(count):
+                        for t in range(PACK):
+                            nc.scalar.activation(
+                                pairs[:, t // 2, j * C : (j + 1) * C, t % 2],
+                                rounded[:, t, :].indirect(offs_t[:, (e0 + j) * (C // 16) : (e0 + j + 1) * (C // 16)]),
+                                COPY,
+                            )
+
+        def join_pairs(g):
+            for g2, a, e0, count, col, pairs in runs:
+                if g2 == g:
+                    nc.vector.tensor_copy(
+                        grouped[g][:, col * PACK : (col + count * C) * PACK].rearrange("p (n u h) -> p n u h", u=2, h=2),
+                        pairs[:].rearrange("p u n h -> p n u h"),
+                    )
 
         def multiply(g, a, e, col):
             nc.tensor.matmul_mx(
@@ -128,10 +133,10 @@ def tile_routed_moe_kernel(tc, xT, w_words, w_scales, gate, offs, pos1, pos2, ou
             )
             passes_done[e] += 1
             if passes_done[e] == PASSES:
-                if e in Y_COPY_ON_SCALAR:
-                    nc.scalar.copy(y[:, e * C : (e + 1) * C], acc[e][:])
-                else:
+                if e in Y_COPY_ON_VECTOR:
                     nc.vector.tensor_copy(y[:, e * C : (e + 1) * C], acc[e][:])
+                else:
+                    nc.scalar.copy(y[:, e * C : (e + 1) * C], acc[e][:])
 
         def quantise(g):
             nc.vector.quantize_mx(out=x_code[g][:].bitcast(FP8X4), scales=x_scale[g][:], in_=grouped[g][:])
@@ -139,35 +144,41 @@ def tile_routed_moe_kernel(tc, xT, w_words, w_scales, gate, offs, pos1, pos2, ou
                 a, lo, hi = GROUPS[g][0]
                 for e in range(lo // C, hi // C):
                     multiply(g, a, e, e * C - lo)
-            for g2, a, e, col in scalar_share:
+            for g2, a, e0, count, col, pairs in runs:
                 if g2 == g:
-                    multiply(g, a, e, col)
+                    for j in range(count):
+                        multiply(g, a, e0 + j, col + j * C)
 
         g4_of = {}
 
         def gather(k):
             a, lo, hi = CUTS[k]
-            i = [pair[0] for pair in PASS_PAIRS].index(a)
-            g4 = ring.tile([P, PACK, hi - lo], F32, name="g4")
+            i, half = where[a]
+            g4 = keep.tile([P, PACK, hi - lo], F32, name="g4")
             for t in range(PACK):
                 nc.vector.tensor_copy(g4[:, t, :], two_planes[i][t][:].rearrange("p h n -> p (h n)").indirect(offs_t[:, lo // 16 : hi // 16]))
             g4_of[k] = g4
 
-        def interleave(k):
+        def interleave(k, g):
             nc.vector.tensor_copy(
-                grouped[k][:, 0 : v_width(k) * PACK].rearrange("p (n t) -> p n t", t=PACK),
+                grouped[g][:, 0 : v_width(g) * PACK].rearrange("p (n t) -> p n t", t=PACK),
                 g4_of[k][:].rearrange("p t n -> p n t"),
             )
 
-        n_cuts = len(CUTS)
-        for k in range(n_cuts + 2):
-            if k < n_cuts:
-                gather(k)
-            if 1 <= k <= n_cuts:
-                interleave(k - 1)
-            if k >= 2:
-                quantise(k - 2)
-        for g in range(n_cuts, n_groups):
+        gather(0)
+        interleave(0, 0)
+        gather(1)
+        quantise(0)
+        interleave(1, 1)
+        join_pairs(1)
+        gather(2)
+        quantise(1)
+        interleave(2, 3)
+        join_pairs(2)
+        quantise(2)
+        quantise(3)
+        for g in (4, 5, 6, 7):
+            join_pairs(g)
             quantise(g)
 
         first = keep.tile([P, T], F32, name="first")

@@ -22,19 +22,20 @@ PASSES = K // (P * PACK)
 SLOTS = E * C
 
 PASS_PAIRS = ((0, 3), (1, 2))
-CUTS = ((0, 0, 512), (0, 512, 1024), (1, 768, 1024))
+CUTS = ((0, 0, 512), (0, 512, 1024), (1, 512, 1024))
 S_PASSES = (3, 2, 1)
 GROUPS = (
     ((0, 0, 512), ()),
     ((0, 512, 1024), ((3, 0, 4),)),
     (None, ((3, 4, 4), (2, 0, 4))),
-    ((1, 768, 1024), ()),
+    ((1, 512, 1024), ()),
     (None, ((2, 4, 4),)),
-    (None, ((1, 0, 4),)),
-    (None, ((1, 4, 1),)),
-    (None, ((1, 5, 1),)),
+    (None, ((1, 0, 2),)),
+    (None, ((1, 2, 1),)),
+    (None, ((1, 3, 1),)),
 )
-Y_COPY_ON_VECTOR = (5, 6, 7)
+Y_COPY_ON_VECTOR = (2, 3)
+RUN = 4
 
 
 def tile_routed_moe_kernel(tc, xT, w_words, w_scales, gate, offs, pos1, pos2, out):
@@ -161,8 +162,8 @@ def tile_routed_moe_kernel(tc, xT, w_words, w_scales, gate, offs, pos1, pos2, ou
 
         def interleave(k, g):
             nc.vector.tensor_copy(
-                grouped[g][:, 0 : v_width(g) * PACK].rearrange("p (n t) -> p n t", t=PACK),
-                g4_of[k][:].rearrange("p t n -> p n t"),
+                grouped[g][:, 0 : v_width(g) * PACK].rearrange("p (c i t) -> p c t i", i=RUN, t=PACK),
+                g4_of[k][:].rearrange("p t (c i) -> p c t i", i=RUN),
             )
 
         gather(0)

@@ -22,19 +22,30 @@ PASSES = K // (P * PACK)
 SLOTS = E * C
 
 PASS_PAIRS = ((0, 3), (1, 2))
-CUTS = ((0, 0, 512), (0, 512, 1024), (1, 512, 1024))
-S_PASSES = (3, 2, 1)
+CUTS = ((0, 0, 512), (0, 512, 1024), (1, 384, 1024))
+G4_BUFS = 1
+LOADS = ((3, 0), (0, 0), (3, 1), (0, 1), (3, 2), (0, 2), (3, 3), (0, 3), (2, 0), (1, 0), (2, 1), (1, 1), (2, 2), (1, 2), (2, 3), (1, 3))
+W_LOADS = (0, 3, 2, 1)
+S_RUNS = (("pairs_a", 3, 0, 4), ("pairs_b", 3, 4, 4), ("pairs_c", 2, 0, 4), ("pairs_d", 2, 4, 4), ("pairs_e", 1, 0, 1), ("pairs_f", 1, 1, 1), ("pairs_g", 1, 2, 1))
 GROUPS = (
-    ((0, 0, 512), ()),
-    ((0, 512, 1024), ((3, 0, 4),)),
-    (None, ((3, 4, 4), (2, 0, 4))),
-    ((1, 512, 1024), ()),
-    (None, ((2, 4, 4),)),
-    (None, ((1, 0, 2),)),
-    (None, ((1, 2, 1),)),
-    (None, ((1, 3, 1),)),
+    (("v", 0, 0, 512),),
+    (("v", 1, 512, 1024), ("s", 0, 0, 4)),
+    (("s", 1, 0, 4), ("s", 2, 0, 4)),
+    (("v", 2, 512, 1024),),
+    (("s", 3, 0, 4),),
+    (("v", 2, 384, 512), ("s", 4, 0, 1)),
+    (("s", 5, 0, 1),),
+    (("s", 6, 0, 1),),
 )
-Y_COPY_ON_VECTOR = (2, 3)
+ORDER = (
+    ("casts", 3), ("scalar", 0), ("scalar", 1),
+    ("planes", (0, 0, 4)), ("interleave", 0),
+    ("casts", 2), ("scalar", 2), ("scalar", 3), ("casts", 1), ("scalar", 4), ("scalar", 5), ("scalar", 6),
+    ("quantise", 0), ("planes", (1, 0, 4)), ("interleave", 1), ("join", 1), ("quantise", 1),
+    ("planes", (2, 0, 4)), ("join", 2), ("interleave", 3), ("quantise", 2), ("join", 4), ("quantise", 3), ("interleave", 5), ("quantise", 4),
+    ("join", 5), ("join", 6), ("quantise", 5), ("join", 7), ("quantise", 6), ("quantise", 7),
+)
+Y_COPY_ON_VECTOR = (0, 1, 2)
 RUN = 4
 
 
@@ -43,6 +54,7 @@ def tile_routed_moe_kernel(tc, xT, w_words, w_scales, gate, offs, pos1, pos2, ou
     with ExitStack() as ctx:
         lists = ctx.enter_context(tc.tile_pool(name="lists", bufs=1))
         keep = ctx.enter_context(tc.tile_pool(name="keep", bufs=1))
+        ring = ctx.enter_context(tc.tile_pool(name="ring", bufs=G4_BUFS))
         psum = ctx.enter_context(tc.psum_pool(name="psum", bufs=1))
 
         offs_t = lists.tile([P, SLOTS // 16], U16, name="offs_t")
@@ -61,16 +73,15 @@ def tile_routed_moe_kernel(tc, xT, w_words, w_scales, gate, offs, pos1, pos2, ou
             for h in range(2):
                 where[PASS_PAIRS[i][h]] = (i, h)
 
-        for i in range(len(PASS_PAIRS)):
-            for t in range(PACK):
-                for h in (1, 0):
-                    nc.sync.dma_start(two_planes[i][t][:, h, :], x_planes[PASS_PAIRS[i][h], :, t, :])
+        for a, t in LOADS:
+            i, h = where[a]
+            nc.sync.dma_start(two_planes[i][t][:, h, :], x_planes[a, :, t, :])
         for q in range(4):
             nc.sync.dma_start(
                 w_scale_t[32 * q : 32 * q + 4, :, :].bitcast(I32),
                 w_scales[:, :, 4 * q : 4 * q + 4, :].rearrange("e a r n -> r (e a) n").bitcast(I32),
             )
-        for a in (0, 3, 2, 1):
+        for a in W_LOADS:
             nc.sync.dma_start(w_code_t[a][:], w_words[:, a].rearrange("e p n r -> p e (n r)").bitcast(I32))
         nc.sync.dma_start(pos1_t[:], pos1)
         nc.sync.dma_start(pos2_t[:], pos2)
@@ -82,44 +93,57 @@ def tile_routed_moe_kernel(tc, xT, w_words, w_scales, gate, offs, pos1, pos2, ou
         y = keep.tile([P, SLOTS], F32, name="y")
         passes_done = [0] * E
 
-        def v_width(g):
-            return 0 if GROUPS[g][0] is None else GROUPS[g][0][2] - GROUPS[g][0][1]
+        def piece_width(piece):
+            return piece[3] - piece[2] if piece[0] == "v" else piece[3] * C
 
         n_groups = len(GROUPS)
-        widths = [v_width(g) + C * sum(run[2] for run in GROUPS[g][1]) for g in range(n_groups)]
+        widths = [sum(piece_width(piece) for piece in GROUPS[g]) for g in range(n_groups)]
         grouped = [keep.tile([P, widths[g] * PACK], BF16, name="grouped%d" % g, align_bytes=64) for g in range(n_groups)]
         x_code = [keep.tile([P, widths[g]], U32, name="x_code%d" % g, align_bytes=64) for g in range(n_groups)]
         x_scale = [keep.tile([P, widths[g]], U8, name="x_scale%d" % g, align_bytes=64) for g in range(n_groups)]
-
-        runs = []
+        first_col = []
         for g in range(n_groups):
-            col = v_width(g)
-            for a, e0, count in GROUPS[g][1]:
-                pairs = keep.tile([P, 2, count * C, 2], BF16, name="pairs%d_%d" % (a, e0))
-                runs.append((g, a, e0, count, col, pairs))
-                col += count * C
+            col = 0
+            row = []
+            for piece in GROUPS[g]:
+                row.append(col)
+                col += piece_width(piece)
+            first_col.append(row)
 
-        for s_pass in S_PASSES:
-            i, half = where[s_pass]
-            rounded = keep.tile([P, PACK, T], BF16, name="rounded%d" % s_pass)
+        rounded = {}
+        pairs_of = {}
+        g4_of = {}
+
+        def casts(a):
+            i, half = where[a]
+            rounded[a] = keep.tile([P, PACK, T], BF16, name="rounded%d" % a)
             for t in range(PACK):
-                nc.vector.tensor_copy(rounded[:, t, :], two_planes[i][t][:, half, :])
-            for g, a, e0, count, col, pairs in runs:
-                if a == s_pass:
-                    for j in range(count):
-                        for t in range(PACK):
-                            nc.scalar.activation(
-                                pairs[:, t // 2, j * C : (j + 1) * C, t % 2],
-                                rounded[:, t, :].indirect(offs_t[:, (e0 + j) * (C // 16) : (e0 + j + 1) * (C // 16)]),
-                                COPY,
-                            )
+                nc.vector.tensor_copy(rounded[a][:, t, :], two_planes[i][t][:, half, :])
+
+        def scalar_run(r):
+            tag, a, e0, count = S_RUNS[r]
+            whole = None
+            if tag == "direct":
+                for g in range(n_groups):
+                    for piece, col in zip(GROUPS[g], first_col[g]):
+                        if piece[0] == "d" and piece[1] == r:
+                            whole = grouped[g][:, col * PACK : (col + count * C) * PACK].rearrange("p (n t) -> p n t", t=PACK)
+            else:
+                pairs_of[r] = keep.tile([P, 2, count * C, 2], BF16, name=tag)
+            for j in range(count):
+                for t in range(PACK):
+                    nc.scalar.activation(
+                        whole[:, j * C : (j + 1) * C, t] if tag == "direct" else pairs_of[r][:, t // 2, j * C : (j + 1) * C, t % 2],
+                        rounded[a][:, t, :].indirect(offs_t[:, (e0 + j) * (C // 16) : (e0 + j + 1) * (C // 16)]),
+                        COPY,
+                    )
 
         def join_pairs(g):
-            for g2, a, e0, count, col, pairs in runs:
-                if g2 == g:
+            for piece, col in zip(GROUPS[g], first_col[g]):
+                if piece[0] == "s":
                     nc.vector.tensor_copy(
-                        grouped[g][:, col * PACK : (col + count * C) * PACK].rearrange("p (n u h) -> p n u h", u=2, h=2),
-                        pairs[:].rearrange("p u n h -> p n u h"),
+                        grouped[g][:, col * PACK : (col + piece[3] * C) * PACK].rearrange("p (n u h) -> p n u h", u=2, h=2),
+                        pairs_of[piece[1]][:, :, piece[2] * C : (piece[2] + piece[3]) * C, :].rearrange("p u n h -> p n u h"),
                     )
 
         def multiply(g, a, e, col):
@@ -141,51 +165,47 @@ def tile_routed_moe_kernel(tc, xT, w_words, w_scales, gate, offs, pos1, pos2, ou
 
         def quantise(g):
             nc.vector.quantize_mx(out=x_code[g][:].bitcast(FP8X4), scales=x_scale[g][:], in_=grouped[g][:])
-            if GROUPS[g][0] is not None:
-                a, lo, hi = GROUPS[g][0]
-                for e in range(lo // C, hi // C):
-                    multiply(g, a, e, e * C - lo)
-            for g2, a, e0, count, col, pairs in runs:
-                if g2 == g:
-                    for j in range(count):
-                        multiply(g, a, e0 + j, col + j * C)
+            for piece, col in zip(GROUPS[g], first_col[g]):
+                if piece[0] == "v":
+                    for e in range(piece[2] // C, piece[3] // C):
+                        multiply(g, CUTS[piece[1]][0], e, col + e * C - piece[2])
+                else:
+                    tag, a, e0, count = S_RUNS[piece[1]]
+                    for j in range(piece[3]):
+                        multiply(g, a, e0 + piece[2] + j, col + j * C)
 
-        g4_of = {}
-
-        def gather(k):
+        def gather_planes(which):
+            k, t0, t1 = which
             a, lo, hi = CUTS[k]
             i, half = where[a]
-            g4 = keep.tile([P, PACK, hi - lo], F32, name="g4")
-            for t in range(PACK):
-                nc.vector.tensor_copy(g4[:, t, :], two_planes[i][t][:].rearrange("p h n -> p (h n)").indirect(offs_t[:, lo // 16 : hi // 16]))
-            g4_of[k] = g4
+            if k not in g4_of:
+                g4_of[k] = ring.tile([P, PACK, hi - lo], F32, name="g4")
+            for t in range(t0, t1):
+                nc.vector.tensor_copy(g4_of[k][:, t, :], two_planes[i][t][:].rearrange("p h n -> p (h n)").indirect(offs_t[:, lo // 16 : hi // 16]))
 
-        def interleave(k, g):
-            nc.vector.tensor_copy(
-                grouped[g][:, 0 : v_width(g) * PACK].rearrange("p (c i t) -> p c t i", i=RUN, t=PACK),
-                g4_of[k][:].rearrange("p t (c i) -> p c t i", i=RUN),
-            )
+        def interleave(g):
+            for piece, col in zip(GROUPS[g], first_col[g]):
+                if piece[0] == "v":
+                    lo = piece[2] - CUTS[piece[1]][1]
+                    hi = piece[3] - CUTS[piece[1]][1]
+                    nc.vector.tensor_copy(
+                        grouped[g][:, col * PACK : (col + hi - lo) * PACK].rearrange("p (c i t) -> p c t i", i=RUN, t=PACK),
+                        g4_of[piece[1]][:, :, lo:hi].rearrange("p t (c i) -> p c t i", i=RUN),
+                    )
 
-        gather(0)
-        interleave(0, 0)
-        gather(1)
-        quantise(0)
-        interleave(1, 1)
-        join_pairs(1)
-        gather(2)
-        quantise(1)
-        interleave(2, 3)
-        join_pairs(2)
-        quantise(2)
-        quantise(3)
-        for g in (4, 5, 6, 7):
-            join_pairs(g)
-            quantise(g)
+        steps = {"casts": casts, "scalar": scalar_run, "planes": gather_planes, "interleave": interleave, "join": join_pairs, "quantise": quantise}
+        for what, which in ORDER:
+            steps[what](which)
 
         first = keep.tile([P, T], F32, name="first")
         second = keep.tile([P, T], F32, name="second")
         result = keep.tile([P, T], F32, name="result")
+        HALF = T // 2
         nc.vector.tensor_tensor(first[:], y[:].indirect(pos1_t[:]), gate_t[0][:], MULT)
-        nc.vector.tensor_tensor(second[:], y[:].indirect(pos2_t[:]), gate_t[1][:], MULT)
-        nc.vector.tensor_tensor(result[:], first[:], second[:], ADD)
-        nc.sync.dma_start(out, result[:])
+        for h in range(2):
+            cols = slice(h * HALF, (h + 1) * HALF)
+            nc.vector.tensor_tensor(second[:, cols], y[:].indirect(pos2_t[:, h * (HALF // 16) : (h + 1) * (HALF // 16)]), gate_t[1][:, cols], MULT)
+        for h in range(2):
+            cols = slice(h * HALF, (h + 1) * HALF)
+            nc.vector.tensor_tensor(result[:, cols], first[:, cols], second[:, cols], ADD)
+            nc.sync.dma_start(out[:, cols], result[:, cols])

@@ -26,14 +26,14 @@ CUTS = ((0, 0, 512), (0, 512, 1024), (1, 384, 1024))
 G4_BUFS = 1
 LOADS = ((3, 0), (0, 0), (3, 1), (0, 1), (3, 2), (0, 2), (3, 3), (0, 3), (2, 0), (1, 0), (2, 1), (1, 1), (2, 2), (1, 2), (2, 3), (1, 3))
 W_LOADS = (0, 3, 2, 1)
-S_RUNS = (("pairs_a", 3, 0, 4), ("pairs_b", 3, 4, 4), ("pairs_c", 2, 0, 4), ("pairs_d", 2, 4, 4), ("pairs_e", 1, 0, 1), ("pairs_f", 1, 1, 1), ("pairs_g", 1, 2, 1))
+S_RUNS = (("pairs_a", 3, 0, 4), ("pairs_b", 3, 4, 4), ("pairs_c", 2, 0, 4), ("pairs_d", 2, 4, 4), ("direct", 1, 0, 1), ("pairs_f", 1, 1, 1), ("pairs_g", 1, 2, 1))
 GROUPS = (
     (("v", 0, 0, 512),),
     (("v", 1, 512, 1024), ("s", 0, 0, 4)),
     (("s", 1, 0, 4), ("s", 2, 0, 4)),
     (("v", 2, 512, 1024),),
     (("s", 3, 0, 4),),
-    (("v", 2, 384, 512), ("s", 4, 0, 1)),
+    (("v", 2, 384, 512), ("d", 4, 0, 1)),
     (("s", 5, 0, 1),),
     (("s", 6, 0, 1),),
 )
@@ -43,9 +43,9 @@ ORDER = (
     ("casts", 2), ("scalar", 2), ("scalar", 3), ("casts", 1), ("scalar", 4), ("scalar", 5), ("scalar", 6),
     ("quantise", 0), ("planes", (1, 0, 4)), ("interleave", 1), ("join", 1), ("quantise", 1),
     ("planes", (2, 0, 4)), ("join", 2), ("interleave", 3), ("quantise", 2), ("join", 4), ("quantise", 3), ("interleave", 5), ("quantise", 4),
-    ("join", 5), ("join", 6), ("quantise", 5), ("join", 7), ("quantise", 6), ("quantise", 7),
+    ("join", 6), ("quantise", 5), ("join", 7), ("quantise", 6), ("quantise", 7),
 )
-Y_COPY_ON_VECTOR = (0, 1, 2)
+Y_COPY_ON_VECTOR = (0, 1)
 RUN = 4
 
 

@@ -40,7 +40,7 @@ GROUPS = (
 ORDER = (
     ("casts", 3), ("scalar", 0), ("scalar", 1),
     ("planes", (0, 0, 4)), ("interleave", 0),
-    ("casts", 2), ("scalar", 2), ("scalar", 3), ("casts", 1), ("scalar", 4), ("scalar", 5), ("scalar", 6),
+    ("casts", 2), ("scalar", 2), ("scalar", 3), ("gcasts", 1), ("scalar", 4), ("scalar", 5), ("scalar", 6),
     ("quantise", 0), ("planes", (1, 0, 4)), ("interleave", 1), ("join", 1), ("quantise", 1),
     ("planes", (2, 0, 4)), ("join", 2), ("interleave", 3), ("quantise", 2), ("join", 4), ("quantise", 3), ("interleave", 5), ("quantise", 4),
     ("join", 6), ("quantise", 5), ("join", 7), ("quantise", 6), ("quantise", 7),
@@ -120,6 +120,12 @@ def tile_routed_moe_kernel(tc, xT, w_words, w_scales, gate, offs, pos1, pos2, ou
             for t in range(PACK):
                 nc.vector.tensor_copy(rounded[a][:, t, :], two_planes[i][t][:, half, :])
 
+        def casts_on_gpsimd(a):
+            i, half = where[a]
+            rounded[a] = keep.tile([P, PACK, T], BF16, name="rounded%d" % a)
+            for t in range(PACK):
+                nc.gpsimd.tensor_copy(rounded[a][:, t, :], two_planes[i][t][:, half, :])
+
         def scalar_run(r):
             tag, a, e0, count = S_RUNS[r]
             whole = None
@@ -193,7 +199,7 @@ def tile_routed_moe_kernel(tc, xT, w_words, w_scales, gate, offs, pos1, pos2, ou
                         g4_of[piece[1]][:, :, lo:hi].rearrange("p t (c i) -> p c t i", i=RUN),
                     )
 
-        steps = {"casts": casts, "scalar": scalar_run, "planes": gather_planes, "interleave": interleave, "join": join_pairs, "quantise": quantise}
+        steps = {"casts": casts, "gcasts": casts_on_gpsimd, "scalar": scalar_run, "planes": gather_planes, "interleave": interleave, "join": join_pairs, "quantise": quantise}
         for what, which in ORDER:
             steps[what](which)
 

@@ -22,27 +22,27 @@ PASSES = K // (P * PACK)
 SLOTS = E * C
 
 PASS_PAIRS = ((0, 3), (1, 2))
-CUTS = ((0, 0, 512), (0, 512, 1024), (1, 384, 1024))
+CUTS = ((0, 0, 512), (0, 512, 1024), (1, 352, 1024))
 G4_BUFS = 1
 LOADS = ((3, 0), (0, 0), (3, 1), (0, 1), (3, 2), (0, 2), (3, 3), (0, 3), (2, 0), (1, 0), (2, 1), (1, 1), (2, 2), (1, 2), (2, 3), (1, 3))
 W_LOADS = (0, 3, 2, 1)
-S_RUNS = (("pairs_a", 3, 0, 4), ("pairs_b", 3, 4, 4), ("pairs_c", 2, 0, 4), ("pairs_d", 2, 4, 4), ("direct", 1, 0, 1), ("pairs_f", 1, 1, 1), ("pairs_g", 1, 2, 1))
+S_RUNS = (("pairs_a", 3, 0, 512), ("pairs_b", 3, 512, 512), ("pairs_c", 2, 0, 512), ("pairs_d", 2, 512, 512), ("direct", 1, 0, 128), ("pairs_f", 1, 128, 128), ("pairs_g", 1, 256, 96))
 GROUPS = (
     (("v", 0, 0, 512),),
-    (("v", 1, 512, 1024), ("s", 0, 0, 4)),
-    (("s", 1, 0, 4), ("s", 2, 0, 4)),
+    (("v", 1, 512, 1024), ("s", 0, 0, 512)),
+    (("s", 1, 0, 512), ("s", 2, 0, 512)),
     (("v", 2, 512, 1024),),
-    (("s", 3, 0, 4),),
-    (("v", 2, 384, 512), ("d", 4, 0, 1)),
-    (("s", 5, 0, 1),),
-    (("s", 6, 0, 1),),
+    (("s", 3, 0, 512),),
+    (("v", 2, 384, 512), ("d", 4, 0, 128)),
+    (("s", 5, 0, 128),),
+    (("s", 6, 0, 96), ("v", 2, 352, 384)),
 )
 ORDER = (
     ("casts", 3), ("scalar", 0), ("scalar", 1),
     ("planes", (0, 0, 4)), ("interleave", 0),
     ("casts", 2), ("scalar", 2), ("scalar", 3), ("gcasts", 1), ("scalar", 4), ("scalar", 5), ("scalar", 6),
     ("quantise", 0), ("planes", (1, 0, 4)), ("interleave", 1), ("join", 1), ("quantise", 1),
-    ("planes", (2, 0, 4)), ("join", 2), ("interleave", 3), ("quantise", 2), ("join", 4), ("quantise", 3), ("interleave", 5), ("quantise", 4),
+    ("planes", (2, 0, 4)), ("join", 2), ("interleave", 3), ("quantise", 2), ("join", 4), ("quantise", 3), ("interleave", 5), ("quantise", 4), ("interleave", 7),
     ("join", 6), ("quantise", 5), ("join", 7), ("quantise", 6), ("quantise", 7),
 )
 Y_COPY_ON_VECTOR = (0, 1)
@@ -94,7 +94,7 @@ def tile_routed_moe_kernel(tc, xT, w_words, w_scales, gate, offs, pos1, pos2, ou
         passes_done = [0] * E
 
         def piece_width(piece):
-            return piece[3] - piece[2] if piece[0] == "v" else piece[3] * C
+            return piece[3] - piece[2] if piece[0] == "v" else piece[3]
 
         n_groups = len(GROUPS)
         widths = [sum(piece_width(piece) for piece in GROUPS[g]) for g in range(n_groups)]
@@ -127,20 +127,21 @@ def tile_routed_moe_kernel(tc, xT, w_words, w_scales, gate, offs, pos1, pos2, ou
                 nc.gpsimd.tensor_copy(rounded[a][:, t, :], two_planes[i][t][:, half, :])
 
         def scalar_run(r):
-            tag, a, e0, count = S_RUNS[r]
+            tag, a, s0, count = S_RUNS[r]
             whole = None
             if tag == "direct":
                 for g in range(n_groups):
                     for piece, col in zip(GROUPS[g], first_col[g]):
                         if piece[0] == "d" and piece[1] == r:
-                            whole = grouped[g][:, col * PACK : (col + count * C) * PACK].rearrange("p (n t) -> p n t", t=PACK)
+                            whole = grouped[g][:, col * PACK : (col + count) * PACK].rearrange("p (n t) -> p n t", t=PACK)
             else:
-                pairs_of[r] = keep.tile([P, 2, count * C, 2], BF16, name=tag)
-            for j in range(count):
+                pairs_of[r] = keep.tile([P, 2, count, 2], BF16, name=tag)
+            for j0 in range(0, count, C):
+                j1 = min(j0 + C, count)
                 for t in range(PACK):
                     nc.scalar.activation(
-                        whole[:, j * C : (j + 1) * C, t] if tag == "direct" else pairs_of[r][:, t // 2, j * C : (j + 1) * C, t % 2],
-                        rounded[a][:, t, :].indirect(offs_t[:, (e0 + j) * (C // 16) : (e0 + j + 1) * (C // 16)]),
+                        whole[:, j0:j1, t] if tag == "direct" else pairs_of[r][:, t // 2, j0:j1, t % 2],
+                        rounded[a][:, t, :].indirect(offs_t[:, (s0 + j0) // 16 : (s0 + j1) // 16]),
                         COPY,
                     )
 
@@ -148,8 +149,8 @@ def tile_routed_moe_kernel(tc, xT, w_words, w_scales, gate, offs, pos1, pos2, ou
             for piece, col in zip(GROUPS[g], first_col[g]):
                 if piece[0] == "s":
                     nc.vector.tensor_copy(
-                        grouped[g][:, col * PACK : (col + piece[3] * C) * PACK].rearrange("p (n u h) -> p n u h", u=2, h=2),
-                        pairs_of[piece[1]][:, :, piece[2] * C : (piece[2] + piece[3]) * C, :].rearrange("p u n h -> p n u h"),
+                        grouped[g][:, col * PACK : (col + piece[3]) * PACK].rearrange("p (n u h) -> p n u h", u=2, h=2),
+                        pairs_of[piece[1]][:, :, piece[2] : piece[2] + piece[3], :].rearrange("p u n h -> p n u h"),
                     )
 
         def multiply(g, a, e, col):
@@ -173,12 +174,14 @@ def tile_routed_moe_kernel(tc, xT, w_words, w_scales, gate, offs, pos1, pos2, ou
             nc.vector.quantize_mx(out=x_code[g][:].bitcast(FP8X4), scales=x_scale[g][:], in_=grouped[g][:])
             for piece, col in zip(GROUPS[g], first_col[g]):
                 if piece[0] == "v":
-                    for e in range(piece[2] // C, piece[3] // C):
-                        multiply(g, CUTS[piece[1]][0], e, col + e * C - piece[2])
+                    a, lo, hi = CUTS[piece[1]][0], piece[2], piece[3]
                 else:
-                    tag, a, e0, count = S_RUNS[piece[1]]
-                    for j in range(piece[3]):
-                        multiply(g, a, e0 + piece[2] + j, col + j * C)
+                    a = S_RUNS[piece[1]][1]
+                    lo = S_RUNS[piece[1]][2] + piece[2]
+                    hi = lo + piece[3]
+                for e in range(E):
+                    if lo <= e * C < hi:
+                        multiply(g, a, e, col + e * C - lo)
 
         def gather_planes(which):
             k, t0, t1 = which

@@ -57,6 +57,11 @@ def tile_routed_moe_kernel(tc, xT, w_words, w_scales, gate, offs, pos1, pos2, ou
         ring = ctx.enter_context(tc.tile_pool(name="ring", bufs=G4_BUFS))
         psum = ctx.enter_context(tc.psum_pool(name="psum", bufs=1))
 
+        warm_in = keep.tile([P, 1], F32, name="warm_in")
+        warm_out = keep.tile([P, 1], F32, name="warm_out")
+        nc.vector.memset(warm_in[:], 0.0)
+        nc.scalar.activation(warm_out[:], warm_in[:], COPY)
+
         offs_t = lists.tile([P, SLOTS // 16], U16, name="offs_t")
         pos1_t = lists.tile([P, T // 16], U16, name="pos1_t")
         pos2_t = lists.tile([P, T // 16], U16, name="pos2_t")

@@ -22,11 +22,11 @@ PASSES = K // (P * PACK)
 SLOTS = E * C
 
 PASS_PAIRS = ((0, 3), (1, 2))
-CUTS = ((0, 0, 512), (0, 512, 1024), (1, 352, 1024))
-G4_BUFS = 1
+CUTS = ((0, 0, 512), (0, 512, 1024), (1, 320, 1024))
+G4_BUFS = 2
 LOADS = ((3, 0), (0, 0), (3, 1), (0, 1), (3, 2), (0, 2), (3, 3), (0, 3), (2, 0), (1, 0), (2, 1), (1, 1), (2, 2), (1, 2), (2, 3), (1, 3))
 W_LOADS = (0, 3, 2, 1)
-S_RUNS = (("pairs_a", 3, 0, 512), ("pairs_b", 3, 512, 512), ("pairs_c", 2, 0, 512), ("pairs_d", 2, 512, 512), ("direct", 1, 0, 128), ("pairs_f", 1, 128, 128), ("pairs_g", 1, 256, 96))
+S_RUNS = (("pairs_a", 3, 0, 512), ("pairs_b", 3, 512, 512), ("pairs_c", 2, 0, 512), ("pairs_a", 2, 512, 512), ("direct", 1, 0, 128), ("pairs_f", 1, 128, 128), ("pairs_g", 1, 256, 64))
 GROUPS = (
     (("v", 0, 0, 512),),
     (("v", 1, 512, 1024), ("s", 0, 0, 512)),
@@ -35,16 +35,18 @@ GROUPS = (
     (("s", 3, 0, 512),),
     (("v", 2, 384, 512), ("d", 4, 0, 128)),
     (("s", 5, 0, 128),),
-    (("s", 6, 0, 96), ("v", 2, 352, 384)),
+    (("s", 6, 0, 64), ("v", 2, 320, 384)),
 )
 ORDER = (
-    ("casts", 3), ("scalar", 0), ("scalar", 1),
+    ("casts", (3, 0, 1)), ("gcasts", (3, 1, 4)), ("scalar", 0), ("scalar", 1),
     ("planes", (0, 0, 4)), ("interleave", 0),
-    ("casts", 2), ("scalar", 2), ("scalar", 3), ("gcasts", 1), ("scalar", 4), ("scalar", 5), ("scalar", 6),
-    ("quantise", 0), ("planes", (1, 0, 4)), ("interleave", 1), ("join", 1), ("quantise", 1),
-    ("planes", (2, 0, 4)), ("join", 2), ("interleave", 3), ("quantise", 2), ("join", 4), ("quantise", 3), ("interleave", 5), ("quantise", 4), ("interleave", 7),
+    ("gcasts", (2, 0, 4)), ("scalar", 2),
+    ("planes", (1, 0, 1)), ("quantise", 0), ("planes", (1, 1, 4)), ("interleave", 1), ("planes", (2, 0, 1)), ("join", 1), ("planes", (2, 1, 2)), ("quantise", 1),
+    ("scalar", 3), ("gcasts", (1, 0, 4)), ("scalar", 4), ("scalar", 5), ("scalar", 6),
+    ("planes", (2, 2, 4)), ("join", (2, 0)), ("interleave", 3), ("join", (2, 1)), ("quantise", 3), ("quantise", 2), ("join", 4), ("interleave", 5), ("quantise", 4), ("interleave", 7),
     ("join", 6), ("quantise", 5), ("join", 7), ("quantise", 6), ("quantise", 7),
 )
+HELD = {"grouped0": 0, "grouped1": 0, "rounded1": 0, "grouped2": 4096}
 Y_COPY_ON_VECTOR = (0, 1)
 RUN = 4
 
@@ -55,6 +57,7 @@ def tile_routed_moe_kernel(tc, xT, w_words, w_scales, gate, offs, pos1, pos2, ou
         lists = ctx.enter_context(tc.tile_pool(name="lists", bufs=1))
         keep = ctx.enter_context(tc.tile_pool(name="keep", bufs=1))
         ring = ctx.enter_context(tc.tile_pool(name="ring", bufs=G4_BUFS))
+        hold = ctx.enter_context(tc.tile_pool(name="hold", bufs=1))
         psum = ctx.enter_context(tc.psum_pool(name="psum", bufs=1))
 
         warm_in = keep.tile([P, 1], F32, name="warm_in")
@@ -103,7 +106,18 @@ def tile_routed_moe_kernel(tc, xT, w_words, w_scales, gate, offs, pos1, pos2, ou
 
         n_groups = len(GROUPS)
         widths = [sum(piece_width(piece) for piece in GROUPS[g]) for g in range(n_groups)]
-        grouped = [keep.tile([P, widths[g] * PACK], BF16, name="grouped%d" % g, align_bytes=64) for g in range(n_groups)]
+        grouped = {}
+
+        def placed(shape, name):
+            if name in HELD:
+                return hold.tile(shape, BF16, name=name, align_bytes=64, offset=HELD[name])
+            return keep.tile(shape, BF16, name=name, align_bytes=64)
+
+        def grouped_tile(g):
+            if g not in grouped:
+                grouped[g] = placed([P, widths[g] * PACK], "grouped%d" % g)
+            return grouped[g]
+
         x_code = [keep.tile([P, widths[g]], U32, name="x_code%d" % g, align_bytes=64) for g in range(n_groups)]
         x_scale = [keep.tile([P, widths[g]], U8, name="x_scale%d" % g, align_bytes=64) for g in range(n_groups)]
         first_col = []
@@ -119,17 +133,22 @@ def tile_routed_moe_kernel(tc, xT, w_words, w_scales, gate, offs, pos1, pos2, ou
         pairs_of = {}
         g4_of = {}
 
-        def casts(a):
-            i, half = where[a]
-            rounded[a] = keep.tile([P, PACK, T], BF16, name="rounded%d" % a)
-            for t in range(PACK):
-                nc.vector.tensor_copy(rounded[a][:, t, :], two_planes[i][t][:, half, :])
+        def rounded_tile(a):
+            if a not in rounded:
+                rounded[a] = placed([P, PACK, T], "rounded%d" % a)
+            return rounded[a]
 
-        def casts_on_gpsimd(a):
+        def casts(which):
+            a, t0, t1 = which
             i, half = where[a]
-            rounded[a] = keep.tile([P, PACK, T], BF16, name="rounded%d" % a)
-            for t in range(PACK):
-                nc.gpsimd.tensor_copy(rounded[a][:, t, :], two_planes[i][t][:, half, :])
+            for t in range(t0, t1):
+                nc.vector.tensor_copy(rounded_tile(a)[:, t, :], two_planes[i][t][:, half, :])
+
+        def casts_on_gpsimd(which):
+            a, t0, t1 = which
+            i, half = where[a]
+            for t in range(t0, t1):
+                nc.gpsimd.tensor_copy(rounded_tile(a)[:, t, :], two_planes[i][t][:, half, :])
 
         def scalar_run(r):
             tag, a, s0, count = S_RUNS[r]
@@ -138,7 +157,7 @@ def tile_routed_moe_kernel(tc, xT, w_words, w_scales, gate, offs, pos1, pos2, ou
                 for g in range(n_groups):
                     for piece, col in zip(GROUPS[g], first_col[g]):
                         if piece[0] == "d" and piece[1] == r:
-                            whole = grouped[g][:, col * PACK : (col + count) * PACK].rearrange("p (n t) -> p n t", t=PACK)
+                            whole = grouped_tile(g)[:, col * PACK : (col + count) * PACK].rearrange("p (n t) -> p n t", t=PACK)
             else:
                 pairs_of[r] = keep.tile([P, 2, count, 2], BF16, name=tag)
             for j0 in range(0, count, C):
@@ -150,11 +169,12 @@ def tile_routed_moe_kernel(tc, xT, w_words, w_scales, gate, offs, pos1, pos2, ou
                         COPY,
                     )
 
-        def join_pairs(g):
-            for piece, col in zip(GROUPS[g], first_col[g]):
-                if piece[0] == "s":
+        def join_pairs(which):
+            g, only = which if isinstance(which, tuple) else (which, None)
+            for k, (piece, col) in enumerate(zip(GROUPS[g], first_col[g])):
+                if piece[0] == "s" and only in (None, k):
                     nc.vector.tensor_copy(
-                        grouped[g][:, col * PACK : (col + piece[3]) * PACK].rearrange("p (n u h) -> p n u h", u=2, h=2),
+                        grouped_tile(g)[:, col * PACK : (col + piece[3]) * PACK].rearrange("p (n u h) -> p n u h", u=2, h=2),
                         pairs_of[piece[1]][:, :, piece[2] : piece[2] + piece[3], :].rearrange("p u n h -> p n u h"),
                     )
 
@@ -176,7 +196,7 @@ def tile_routed_moe_kernel(tc, xT, w_words, w_scales, gate, offs, pos1, pos2, ou
                     nc.scalar.copy(y[:, e * C : (e + 1) * C], acc[e][:])
 
         def quantise(g):
-            nc.vector.quantize_mx(out=x_code[g][:].bitcast(FP8X4), scales=x_scale[g][:], in_=grouped[g][:])
+            nc.vector.quantize_mx(out=x_code[g][:].bitcast(FP8X4), scales=x_scale[g][:], in_=grouped_tile(g)[:])
             for piece, col in zip(GROUPS[g], first_col[g]):
                 if piece[0] == "v":
                     a, lo, hi = CUTS[piece[1]][0], piece[2], piece[3]
@@ -203,7 +223,7 @@ def tile_routed_moe_kernel(tc, xT, w_words, w_scales, gate, offs, pos1, pos2, ou
                     lo = piece[2] - CUTS[piece[1]][1]
                     hi = piece[3] - CUTS[piece[1]][1]
                     nc.vector.tensor_copy(
-                        grouped[g][:, col * PACK : (col + hi - lo) * PACK].rearrange("p (c i t) -> p c t i", i=RUN, t=PACK),
+                        grouped_tile(g)[:, col * PACK : (col + hi - lo) * PACK].rearrange("p (c i t) -> p c t i", i=RUN, t=PACK),
                         g4_of[piece[1]][:, :, lo:hi].rearrange("p t (c i) -> p c t i", i=RUN),
                     )
 

@@ -24,29 +24,29 @@ SLOTS = E * C
 PASS_PAIRS = ((0, 3), (1, 2))
 CUTS = ((0, 0, 512), (0, 512, 1024), (1, 320, 1024))
 G4_BUFS = 2
-LOADS = ((3, 0), (0, 0), (3, 1), (0, 1), (3, 2), (0, 2), (3, 3), (0, 3), (2, 0), (1, 0), (2, 1), (1, 1), (2, 2), (1, 2), (2, 3), (1, 3))
+LOADS = ((3, 0), (0, 0), (3, 1), (0, 1), (2, 0), (3, 2), (0, 2), (2, 1), (3, 3), (0, 3), (2, 2), (2, 3), (1, 0), (1, 1), (1, 2), (1, 3))
 W_LOADS = (0, 3, 2, 1)
-S_RUNS = (("pairs_a", 3, 0, 512), ("pairs_b", 3, 512, 512), ("pairs_c", 2, 0, 512), ("pairs_a", 2, 512, 512), ("direct", 1, 0, 128), ("pairs_f", 1, 128, 128), ("pairs_g", 1, 256, 64))
+S_RUNS = (("pairs_a", 3, 0, 512), ("pairs_b", 3, 512, 512), ("pairs_c", 2, 0, 512), ("pairs_d", 2, 512, 512), ("pairs_e", 1, 0, 128), ("pairs_f", 1, 128, 128), ("direct", 1, 256, 64))
+PLANE_BY_PLANE = (2,)
 GROUPS = (
     (("v", 0, 0, 512),),
     (("v", 1, 512, 1024), ("s", 0, 0, 512)),
     (("s", 1, 0, 512), ("s", 2, 0, 512)),
     (("v", 2, 512, 1024),),
     (("s", 3, 0, 512),),
-    (("v", 2, 384, 512), ("d", 4, 0, 128)),
+    (("v", 2, 384, 512), ("s", 4, 0, 128)),
     (("s", 5, 0, 128),),
-    (("s", 6, 0, 64), ("v", 2, 320, 384)),
+    (("d", 6, 0, 64), ("v", 2, 320, 384)),
 )
 ORDER = (
-    ("casts", (3, 0, 1)), ("gcasts", (3, 1, 4)), ("scalar", 0), ("scalar", 1),
-    ("planes", (0, 0, 4)), ("interleave", 0),
-    ("gcasts", (2, 0, 4)), ("scalar", 2),
-    ("planes", (1, 0, 1)), ("quantise", 0), ("planes", (1, 1, 4)), ("interleave", 1), ("planes", (2, 0, 1)), ("join", 1), ("planes", (2, 1, 2)), ("quantise", 1),
-    ("scalar", 3), ("gcasts", (1, 0, 4)), ("scalar", 4), ("scalar", 5), ("scalar", 6),
+    ("casts", (3, 0, 4)), ("scalar", 0), ("scalar", 1), ("gcasts", (2, 0, 4)), ("gcasts", (1, 0, 4)),
+    ("planes", (0, 0, 4)), ("interleave", 0), ("planes", (1, 0, 1)), ("quantise", 0),
+    ("scalar", 2), ("scalar", 3), ("scalar", 4), ("scalar", 5), ("scalar", 6),
+    ("planes", (1, 1, 4)), ("interleave", 1), ("planes", (2, 0, 1)), ("join", 1), ("planes", (2, 1, 2)), ("quantise", 1),
     ("planes", (2, 2, 4)), ("join", (2, 0)), ("interleave", 3), ("join", (2, 1)), ("quantise", 3), ("quantise", 2), ("join", 4), ("interleave", 5), ("quantise", 4), ("interleave", 7),
-    ("join", 6), ("quantise", 5), ("join", 7), ("quantise", 6), ("quantise", 7),
+    ("join", 5), ("join", 6), ("quantise", 5), ("quantise", 6), ("quantise", 7),
 )
-HELD = {"grouped0": 0, "grouped1": 0, "rounded1": 0, "grouped2": 4096}
+HELD = {"pairs_c": 0, "rounded3": 4032, "pairs_d": 8064, "rounded2": 12160, "pairs_e": 12160, "pairs_f": 13184, "grouped7": 14208}
 Y_COPY_ON_VECTOR = (0, 1)
 RUN = 4
 
@@ -159,10 +159,15 @@ def tile_routed_moe_kernel(tc, xT, w_words, w_scales, gate, offs, pos1, pos2, ou
                         if piece[0] == "d" and piece[1] == r:
                             whole = grouped_tile(g)[:, col * PACK : (col + count) * PACK].rearrange("p (n t) -> p n t", t=PACK)
             else:
-                pairs_of[r] = keep.tile([P, 2, count, 2], BF16, name=tag)
-            for j0 in range(0, count, C):
+                pairs_of[r] = placed([P, 2, count, 2], tag)
+            starts = range(0, count, C)
+            if r in PLANE_BY_PLANE:
+                todo = [(j0, t) for t in range(PACK) for j0 in starts]
+            else:
+                todo = [(j0, t) for j0 in starts for t in range(PACK)]
+            for j0, t in todo:
                 j1 = min(j0 + C, count)
-                for t in range(PACK):
+                if True:
                     nc.scalar.activation(
                         whole[:, j0:j1, t] if tag == "direct" else pairs_of[r][:, t // 2, j0:j1, t % 2],
                         rounded[a][:, t, :].indirect(offs_t[:, (s0 + j0) // 16 : (s0 + j1) // 16]),

@@ -22,11 +22,11 @@ PASSES = K // (P * PACK)
 SLOTS = E * C
 
 PASS_PAIRS = ((0, 3), (1, 2))
-CUTS = ((0, 0, 512), (0, 512, 1024), (1, 320, 1024))
+CUTS = ((0, 0, 512), (0, 512, 1024), (1, 352, 1024))
 G4_BUFS = 2
 LOADS = ((3, 0), (0, 0), (3, 1), (0, 1), (2, 0), (3, 2), (0, 2), (2, 1), (3, 3), (0, 3), (2, 2), (2, 3), (1, 0), (1, 1), (1, 2), (1, 3))
 W_LOADS = (0, 3, 2, 1)
-S_RUNS = (("pairs_a", 3, 0, 512), ("pairs_b", 3, 512, 512), ("pairs_c", 2, 0, 512), ("pairs_d", 2, 512, 512), ("pairs_e", 1, 0, 128), ("pairs_f", 1, 128, 128), ("direct", 1, 256, 64))
+S_RUNS = (("pairs_a", 3, 0, 512), ("pairs_b", 3, 512, 512), ("pairs_c", 2, 0, 512), ("pairs_d", 2, 512, 512), ("pairs_e", 1, 0, 128), ("pairs_f", 1, 128, 128), ("direct", 1, 256, 96))
 PLANE_BY_PLANE = (2,)
 GROUPS = (
     (("v", 0, 0, 512),),
@@ -36,18 +36,18 @@ GROUPS = (
     (("s", 3, 0, 512),),
     (("v", 2, 384, 512), ("s", 4, 0, 128)),
     (("s", 5, 0, 128),),
-    (("d", 6, 0, 64), ("v", 2, 320, 384)),
+    (("d", 6, 0, 96), ("v", 2, 352, 384)),
 )
 ORDER = (
     ("casts", (3, 0, 4)), ("scalar", 0), ("scalar", 1), ("gcasts", (2, 0, 4)), ("gcasts", (1, 0, 4)),
     ("planes", (0, 0, 4)), ("interleave", 0), ("planes", (1, 0, 1)), ("quantise", 0),
     ("scalar", 2), ("scalar", 3), ("scalar", 4), ("scalar", 5), ("scalar", 6),
     ("planes", (1, 1, 4)), ("interleave", 1), ("planes", (2, 0, 1)), ("join", 1), ("planes", (2, 1, 2)), ("quantise", 1),
-    ("planes", (2, 2, 4)), ("join", (2, 0)), ("interleave", 3), ("join", (2, 1)), ("quantise", 3), ("quantise", 2), ("join", 4), ("interleave", 5), ("quantise", 4), ("interleave", 7),
-    ("join", 5), ("join", 6), ("quantise", 5), ("quantise", 6), ("quantise", 7),
+    ("planes", (2, 2, 4)), ("join", (2, 0)), ("interleave", 3), ("join", (2, 1)), ("quantise", 3), ("quantise", 2), ("join", 4), ("interleave", 5), ("quantise", 4),
+    ("join", 5), ("join", 6), ("interleave", 7), ("quantise", 5), ("quantise", 6), ("quantise", 7),
 )
 HELD = {"pairs_c": 0, "rounded3": 4032, "pairs_d": 8064, "rounded2": 12160, "pairs_e": 12160, "pairs_f": 13184, "grouped7": 14208}
-Y_COPY_ON_VECTOR = (0, 1)
+Y_COPY_ON_VECTOR = ()
 RUN = 4
 
 

@@ -22,11 +22,11 @@ PASSES = K // (P * PACK)
 SLOTS = E * C
 
 PASS_PAIRS = ((0, 3), (1, 2))
-CUTS = ((0, 0, 512), (0, 512, 1024), (1, 352, 1024))
+CUTS = ((0, 0, 512), (0, 512, 1024), (1, 320, 1024))
 G4_BUFS = 2
 LOADS = ((3, 0), (0, 0), (3, 1), (0, 1), (2, 0), (3, 2), (0, 2), (2, 1), (3, 3), (0, 3), (2, 2), (2, 3), (1, 0), (1, 1), (1, 2), (1, 3))
 W_LOADS = (0, 3, 2, 1)
-S_RUNS = (("pairs_a", 3, 0, 512), ("pairs_b", 3, 512, 512), ("pairs_c", 2, 0, 512), ("pairs_d", 2, 512, 512), ("pairs_e", 1, 0, 128), ("pairs_f", 1, 128, 128), ("direct", 1, 256, 96))
+S_RUNS = (("pairs_a", 3, 0, 512), ("pairs_b", 3, 512, 512), ("pairs_c", 2, 0, 512), ("pairs_d", 2, 512, 512), ("pairs_e", 1, 0, 128), ("pairs_f", 1, 128, 128), ("direct", 1, 256, 64))
 PLANE_BY_PLANE = (2,)
 GROUPS = (
     (("v", 0, 0, 512),),
@@ -36,7 +36,7 @@ GROUPS = (
     (("s", 3, 0, 512),),
     (("v", 2, 384, 512), ("s", 4, 0, 128)),
     (("s", 5, 0, 128),),
-    (("d", 6, 0, 96), ("v", 2, 352, 384)),
+    (("d", 6, 0, 64), ("v", 2, 320, 384)),
 )
 ORDER = (
     ("casts", (3, 0, 4)), ("scalar", 0), ("scalar", 1), ("gcasts", (2, 0, 4)), ("gcasts", (1, 0, 4)),

@@ -47,7 +47,7 @@ ORDER = (
     ("join", 5), ("join", 6), ("interleave", 7), ("quantise", 5), ("quantise", 6), ("quantise", 7),
 )
 HELD = {"pairs_c": 0, "rounded3": 4032, "pairs_d": 8064, "rounded2": 12160, "pairs_e": 12160, "pairs_f": 13184, "grouped7": 14208}
-Y_COPY_ON_VECTOR = ()
+Y_COPY_ON_VECTOR = (0, 1, 3)
 RUN = 4
 
 

@@ -48,7 +48,7 @@ ORDER = (
 )
 HELD = {"pairs_c": 0, "rounded3": 4032, "pairs_d": 8064, "rounded2": 12160, "pairs_e": 12160, "pairs_f": 13184, "grouped7": 14208}
 Y_COPY_ON_VECTOR = (0, 1, 3)
-RUN = 4
+RUN = 8
 
 
 def tile_routed_moe_kernel(tc, xT, w_words, w_scales, gate, offs, pos1, pos2, out):

@@ -22,11 +22,11 @@ PASSES = K // (P * PACK)
 SLOTS = E * C
 
 PASS_PAIRS = ((0, 3), (1, 2))
-CUTS = ((0, 0, 512), (0, 512, 1024), (1, 320, 1024))
+CUTS = ((0, 0, 512), (0, 512, 1024), (1, 352, 1024))
 G4_BUFS = 2
 LOADS = ((3, 0), (0, 0), (3, 1), (0, 1), (2, 0), (3, 2), (0, 2), (2, 1), (3, 3), (0, 3), (2, 2), (2, 3), (1, 0), (1, 1), (1, 2), (1, 3))
 W_LOADS = (0, 3, 2, 1)
-S_RUNS = (("pairs_a", 3, 0, 512), ("pairs_b", 3, 512, 512), ("pairs_c", 2, 0, 512), ("pairs_d", 2, 512, 512), ("pairs_e", 1, 0, 128), ("pairs_f", 1, 128, 128), ("direct", 1, 256, 64))
+S_RUNS = (("pairs_a", 3, 0, 512), ("pairs_b", 3, 512, 512), ("pairs_c", 2, 0, 512), ("pairs_d", 2, 512, 512), ("pairs_e", 1, 0, 128), ("pairs_f", 1, 128, 128), ("direct", 1, 256, 96))
 PLANE_BY_PLANE = (2,)
 GROUPS = (
     (("v", 0, 0, 512),),
@@ -36,7 +36,7 @@ GROUPS = (
     (("s", 3, 0, 512),),
     (("v", 2, 384, 512), ("s", 4, 0, 128)),
     (("s", 5, 0, 128),),
-    (("d", 6, 0, 64), ("v", 2, 320, 384)),
+    (("d", 6, 0, 96), ("v", 2, 352, 384)),
 )
 ORDER = (
     ("casts", (3, 0, 4)), ("scalar", 0), ("scalar", 1), ("gcasts", (2, 0, 4)), ("gcasts", (1, 0, 4)),
@@ -68,7 +68,6 @@ def tile_routed_moe_kernel(tc, xT, w_words, w_scales, gate, offs, pos1, pos2, ou
         offs_t = lists.tile([P, SLOTS // 16], U16, name="offs_t")
         pos1_t = lists.tile([P, T // 16], U16, name="pos1_t")
         pos2_t = lists.tile([P, T // 16], U16, name="pos2_t")
-        nc.sync.dma_start(offs_t[:], offs)
 
         w_scale_t = keep.tile([P, E * PASSES, N], U8, name="w_scale_t", align_bytes=64)
         nc.vector.memset(w_scale_t[:].rearrange("p b n -> p (b n)").bitcast(I32), 0)
@@ -81,9 +80,14 @@ def tile_routed_moe_kernel(tc, xT, w_words, w_scales, gate, offs, pos1, pos2, ou
             for h in range(2):
                 where[PASS_PAIRS[i][h]] = (i, h)
 
-        for a, t in LOADS:
+        for k, (a, t) in enumerate(LOADS):
             i, h = where[a]
-            nc.sync.dma_start(two_planes[i][t][:, h, :], x_planes[a, :, t, :])
+            if k == 0:
+                for c0 in range(0, T, T // 2):
+                    nc.sync.dma_start(two_planes[i][t][:, h, c0 : c0 + T // 2], x_planes[a, :, t, c0 : c0 + T // 2])
+                nc.sync.dma_start(offs_t[:], offs)
+            else:
+                nc.sync.dma_start(two_planes[i][t][:, h, :], x_planes[a, :, t, :])
         for q in range(4):
             nc.sync.dma_start(
                 w_scale_t[32 * q : 32 * q + 4, :, :].bitcast(I32),
@@ -142,7 +146,9 @@ def tile_routed_moe_kernel(tc, xT, w_words, w_scales, gate, offs, pos1, pos2, ou
             a, t0, t1 = which
             i, half = where[a]
             for t in range(t0, t1):
-                nc.vector.tensor_copy(rounded_tile(a)[:, t, :], two_planes[i][t][:, half, :])
+                pieces = 2 if (a, t) == LOADS[0] else 1
+                for c0 in range(0, T, T // pieces):
+                    nc.vector.tensor_copy(rounded_tile(a)[:, t, c0 : c0 + T // pieces], two_planes[i][t][:, half, c0 : c0 + T // pieces])
 
         def casts_on_gpsimd(which):
             a, t0, t1 = which

@@ -42,11 +42,10 @@ ORDER = (
     ("casts", (3, 0, 4)), ("scalar", 0), ("scalar", 1), ("gcasts", (2, 0, 4)), ("gcasts", (1, 0, 4)),
     ("planes", (0, 0, 4)), ("interleave", 0), ("planes", (1, 0, 1)), ("quantise", 0),
     ("scalar", 2), ("scalar", 3), ("scalar", 4), ("scalar", 5), ("scalar", 6),
-    ("planes", (1, 1, 4)), ("interleave", 1), ("planes", (2, 0, 1)), ("join", 1), ("planes", (2, 1, 2)), ("quantise", 1),
-    ("planes", (2, 2, 4)), ("join", (2, 0)), ("interleave", 3), ("join", (2, 1)), ("quantise", 3), ("quantise", 2), ("join", 4), ("interleave", 5), ("quantise", 4),
+    ("planes", (1, 1, 4)), ("interleave", 1), ("planes", (2, 0, 3)), ("join", 1), ("planes", (2, 3, 4)), ("quantise", 1),
+    ("join", (2, 0)), ("interleave", 3), ("join", (2, 1)), ("quantise", 3), ("quantise", 2), ("join", 4), ("interleave", 5), ("quantise", 4),
     ("join", 5), ("join", 6), ("interleave", 7), ("quantise", 5), ("quantise", 6), ("quantise", 7),
 )
-HELD = {"pairs_c": 0, "rounded3": 4032, "pairs_d": 8064, "rounded2": 12160, "pairs_e": 12160, "pairs_f": 13184, "grouped7": 14208}
 Y_COPY_ON_VECTOR = (0, 1, 3)
 RUN = 8
 
@@ -57,7 +56,6 @@ def tile_routed_moe_kernel(tc, xT, w_words, w_scales, gate, offs, pos1, pos2, ou
         lists = ctx.enter_context(tc.tile_pool(name="lists", bufs=1))
         keep = ctx.enter_context(tc.tile_pool(name="keep", bufs=1))
         ring = ctx.enter_context(tc.tile_pool(name="ring", bufs=G4_BUFS))
-        hold = ctx.enter_context(tc.tile_pool(name="hold", bufs=1))
         psum = ctx.enter_context(tc.psum_pool(name="psum", bufs=1))
 
         warm_in = keep.tile([P, 1], F32, name="warm_in")
@@ -113,8 +111,6 @@ def tile_routed_moe_kernel(tc, xT, w_words, w_scales, gate, offs, pos1, pos2, ou
         grouped = {}
 
         def placed(shape, name):
-            if name in HELD:
-                return hold.tile(shape, BF16, name=name, align_bytes=64, offset=HELD[name])
             return keep.tile(shape, BF16, name=name, align_bytes=64)
 
         def grouped_tile(g):

from contextlib import ExitStack

import concourse.mybir as mybir

K, T, E, C, N = 2048, 512, 8, 128, 128
FLOPS = 2 * K * N * E * C

F32 = mybir.dt.float32
BF16 = mybir.dt.bfloat16
I32 = mybir.dt.int32
U32 = mybir.dt.uint32
U16 = mybir.dt.uint16
U8 = mybir.dt.uint8
FP8X4 = mybir.dt.float8_e4m3fn_x4
MULT = mybir.AluOpType.mult
ADD = mybir.AluOpType.add
COPY = mybir.ActivationFunctionType.Copy

P = 128
PACK = 4
PASSES = K // (P * PACK)
SLOTS = E * C

PASS_PAIRS = ((0, 3), (1, 2))
CUTS = ((0, 0, 512), (0, 512, 1024), (1, 352, 1024))
G4_BUFS = 2
LOADS = ((3, 0), (0, 0), (3, 1), (0, 1), (2, 0), (3, 2), (0, 2), (2, 1), (3, 3), (0, 3), (2, 2), (2, 3), (1, 0), (1, 1), (1, 2), (1, 3))
W_LOADS = (0, 3, 2, 1)
S_RUNS = (("pairs_a", 3, 0, 512), ("pairs_b", 3, 512, 512), ("pairs_c", 2, 0, 512), ("pairs_d", 2, 512, 512), ("pairs_e", 1, 0, 128), ("pairs_f", 1, 128, 128), ("direct", 1, 256, 96))
PLANE_BY_PLANE = (2,)
GROUPS = (
    (("v", 0, 0, 512),),
    (("v", 1, 512, 1024), ("s", 0, 0, 512)),
    (("s", 1, 0, 512), ("s", 2, 0, 512)),
    (("v", 2, 512, 1024),),
    (("s", 3, 0, 512),),
    (("v", 2, 384, 512), ("s", 4, 0, 128)),
    (("s", 5, 0, 128),),
    (("d", 6, 0, 96), ("v", 2, 352, 384)),
)
ORDER = (
    ("casts", (3, 0, 4)), ("scalar", 0), ("scalar", 1), ("gcasts", (2, 0, 4)), ("gcasts", (1, 0, 4)),
    ("planes", (0, 0, 4)), ("interleave", 0), ("planes", (1, 0, 1)), ("quantise", 0),
    ("scalar", 2), ("scalar", 3), ("scalar", 4), ("scalar", 5), ("scalar", 6),
    ("planes", (1, 1, 4)), ("interleave", 1), ("planes", (2, 0, 3)), ("join", 1), ("planes", (2, 3, 4)), ("quantise", 1),
    ("join", (2, 0)), ("interleave", 3), ("join", (2, 1)), ("quantise", 3), ("quantise", 2), ("join", 4), ("interleave", 5), ("quantise", 4),
    ("join", 5), ("join", 6), ("interleave", 7), ("quantise", 5), ("quantise", 6), ("quantise", 7),
)
Y_COPY_ON_VECTOR = (0, 1, 3)
RUN = 8


def tile_routed_moe_kernel(tc, xT, w_words, w_scales, gate, offs, pos1, pos2, out):
    nc = tc.nc
    with ExitStack() as ctx:
        lists = ctx.enter_context(tc.tile_pool(name="lists", bufs=1))
        keep = ctx.enter_context(tc.tile_pool(name="keep", bufs=1))
        ring = ctx.enter_context(tc.tile_pool(name="ring", bufs=G4_BUFS))
        psum = ctx.enter_context(tc.psum_pool(name="psum", bufs=1))

        warm_in = keep.tile([P, 1], F32, name="warm_in")
        warm_out = keep.tile([P, 1], F32, name="warm_out")
        nc.vector.memset(warm_in[:], 0.0)
        nc.scalar.activation(warm_out[:], warm_in[:], COPY)

        offs_t = lists.tile([P, SLOTS // 16], U16, name="offs_t")
        pos1_t = lists.tile([P, T // 16], U16, name="pos1_t")
        pos2_t = lists.tile([P, T // 16], U16, name="pos2_t")

        w_scale_t = keep.tile([P, E * PASSES, N], U8, name="w_scale_t", align_bytes=64)
        nc.vector.memset(w_scale_t[:].rearrange("p b n -> p (b n)").bitcast(I32), 0)

        x_planes = xT.rearrange("(a p t) n -> a p t n", p=P, t=PACK)
        two_planes = [[keep.tile([P, 2, T], F32, name="planes%d_%d" % (i, t)) for t in range(PACK)] for i in range(len(PASS_PAIRS))]
        w_code_t = [keep.tile([P, E, N], I32, name="w_code%d" % a, align_bytes=64) for a in range(PASSES)]
        where = {}
        for i in range(len(PASS_PAIRS)):
            for h in range(2):
                where[PASS_PAIRS[i][h]] = (i, h)

        for k, (a, t) in enumerate(LOADS):
            i, h = where[a]
            if k == 0:
                for c0 in range(0, T, T // 2):
                    nc.sync.dma_start(two_planes[i][t][:, h, c0 : c0 + T // 2], x_planes[a, :, t, c0 : c0 + T // 2])
                nc.sync.dma_start(offs_t[:], offs)
            else:
                nc.sync.dma_start(two_planes[i][t][:, h, :], x_planes[a, :, t, :])
        for q in range(4):
            nc.sync.dma_start(
                w_scale_t[32 * q : 32 * q + 4, :, :].bitcast(I32),
                w_scales[:, :, 4 * q : 4 * q + 4, :].rearrange("e a r n -> r (e a) n").bitcast(I32),
            )
        for a in W_LOADS:
            nc.sync.dma_start(w_code_t[a][:], w_words[:, a].rearrange("e p n r -> p e (n r)").bitcast(I32))
        nc.sync.dma_start(pos1_t[:], pos1)
        nc.sync.dma_start(pos2_t[:], pos2)
        gate_t = [keep.tile([P, T], F32, name="gate%d" % r) for r in range(2)]
        for r in range(2):
            nc.sync.dma_start(gate_t[r][:], gate[r])

        acc = [psum.tile([P, C], F32, name="acc%d" % e) for e in range(E)]
        y = keep.tile([P, SLOTS], F32, name="y")
        passes_done = [0] * E

        def piece_width(piece):
            return piece[3] - piece[2] if piece[0] == "v" else piece[3]

        n_groups = len(GROUPS)
        widths = [sum(piece_width(piece) for piece in GROUPS[g]) for g in range(n_groups)]
        grouped = {}

        def placed(shape, name):
            return keep.tile(shape, BF16, name=name, align_bytes=64)

        def grouped_tile(g):
            if g not in grouped:
                grouped[g] = placed([P, widths[g] * PACK], "grouped%d" % g)
            return grouped[g]

        x_code = [keep.tile([P, widths[g]], U32, name="x_code%d" % g, align_bytes=64) for g in range(n_groups)]
        x_scale = [keep.tile([P, widths[g]], U8, name="x_scale%d" % g, align_bytes=64) for g in range(n_groups)]
        first_col = []
        for g in range(n_groups):
            col = 0
            row = []
            for piece in GROUPS[g]:
                row.append(col)
                col += piece_width(piece)
            first_col.append(row)

        rounded = {}
        pairs_of = {}
        g4_of = {}

        def rounded_tile(a):
            if a not in rounded:
                rounded[a] = placed([P, PACK, T], "rounded%d" % a)
            return rounded[a]

        def casts(which):
            a, t0, t1 = which
            i, half = where[a]
            for t in range(t0, t1):
                pieces = 2 if (a, t) == LOADS[0] else 1
                for c0 in range(0, T, T // pieces):
                    nc.vector.tensor_copy(rounded_tile(a)[:, t, c0 : c0 + T // pieces], two_planes[i][t][:, half, c0 : c0 + T // pieces])

        def casts_on_gpsimd(which):
            a, t0, t1 = which
            i, half = where[a]
            for t in range(t0, t1):
                nc.gpsimd.tensor_copy(rounded_tile(a)[:, t, :], two_planes[i][t][:, half, :])

        def scalar_run(r):
            tag, a, s0, count = S_RUNS[r]
            whole = None
            if tag == "direct":
                for g in range(n_groups):
                    for piece, col in zip(GROUPS[g], first_col[g]):
                        if piece[0] == "d" and piece[1] == r:
                            whole = grouped_tile(g)[:, col * PACK : (col + count) * PACK].rearrange("p (n t) -> p n t", t=PACK)
            else:
                pairs_of[r] = placed([P, 2, count, 2], tag)
            starts = range(0, count, C)
            if r in PLANE_BY_PLANE:
                todo = [(j0, t) for t in range(PACK) for j0 in starts]
            else:
                todo = [(j0, t) for j0 in starts for t in range(PACK)]
            for j0, t in todo:
                j1 = min(j0 + C, count)
                if True:
                    nc.scalar.activation(
                        whole[:, j0:j1, t] if tag == "direct" else pairs_of[r][:, t // 2, j0:j1, t % 2],
                        rounded[a][:, t, :].indirect(offs_t[:, (s0 + j0) // 16 : (s0 + j1) // 16]),
                        COPY,
                    )

        def join_pairs(which):
            g, only = which if isinstance(which, tuple) else (which, None)
            for k, (piece, col) in enumerate(zip(GROUPS[g], first_col[g])):
                if piece[0] == "s" and only in (None, k):
                    nc.vector.tensor_copy(
                        grouped_tile(g)[:, col * PACK : (col + piece[3]) * PACK].rearrange("p (n u h) -> p n u h", u=2, h=2),
                        pairs_of[piece[1]][:, :, piece[2] : piece[2] + piece[3], :].rearrange("p u n h -> p n u h"),
                    )

        def multiply(g, a, e, col):
            nc.tensor.matmul_mx(
                out=acc[e][:],
                lhsT=w_code_t[a][:, e, :].bitcast(FP8X4),
                lhsT_scale=w_scale_t[:, e * PASSES + a, :],
                rhs=x_code[g][:, col : col + C].bitcast(FP8X4),
                rhs_scale=x_scale[g][:, col : col + C],
                start=(passes_done[e] == 0),
                stop=(passes_done[e] == PASSES - 1),
            )
            passes_done[e] += 1
            if passes_done[e] == PASSES:
                if e in Y_COPY_ON_VECTOR:
                    nc.vector.tensor_copy(y[:, e * C : (e + 1) * C], acc[e][:])
                else:
                    nc.scalar.copy(y[:, e * C : (e + 1) * C], acc[e][:])

        def quantise(g):
            nc.vector.quantize_mx(out=x_code[g][:].bitcast(FP8X4), scales=x_scale[g][:], in_=grouped_tile(g)[:])
            for piece, col in zip(GROUPS[g], first_col[g]):
                if piece[0] == "v":
                    a, lo, hi = CUTS[piece[1]][0], piece[2], piece[3]
                else:
                    a = S_RUNS[piece[1]][1]
                    lo = S_RUNS[piece[1]][2] + piece[2]
                    hi = lo + piece[3]
                for e in range(E):
                    if lo <= e * C < hi:
                        multiply(g, a, e, col + e * C - lo)

        def gather_planes(which):
            k, t0, t1 = which
            a, lo, hi = CUTS[k]
            i, half = where[a]
            if k not in g4_of:
                g4_of[k] = ring.tile([P, PACK, hi - lo], F32, name="g4")
            for t in range(t0, t1):
                nc.vector.tensor_copy(g4_of[k][:, t, :], two_planes[i][t][:].rearrange("p h n -> p (h n)").indirect(offs_t[:, lo // 16 : hi // 16]))

        def interleave(g):
            for piece, col in zip(GROUPS[g], first_col[g]):
                if piece[0] == "v":
                    lo = piece[2] - CUTS[piece[1]][1]
                    hi = piece[3] - CUTS[piece[1]][1]
                    nc.vector.tensor_copy(
                        grouped_tile(g)[:, col * PACK : (col + hi - lo) * PACK].rearrange("p (c i t) -> p c t i", i=RUN, t=PACK),
                        g4_of[piece[1]][:, :, lo:hi].rearrange("p t (c i) -> p c t i", i=RUN),
                    )

        steps = {"casts": casts, "gcasts": casts_on_gpsimd, "scalar": scalar_run, "planes": gather_planes, "interleave": interleave, "join": join_pairs, "quantise": quantise}
        for what, which in ORDER:
            steps[what](which)

        first = keep.tile([P, T], F32, name="first")
        second = keep.tile([P, T], F32, name="second")
        result = keep.tile([P, T], F32, name="result")
        HALF = T // 2
        nc.vector.tensor_tensor(first[:], y[:].indirect(pos1_t[:]), gate_t[0][:], MULT)
        for h in range(2):
            cols = slice(h * HALF, (h + 1) * HALF)
            nc.vector.tensor_tensor(second[:, cols], y[:].indirect(pos2_t[:, h * (HALF // 16) : (h + 1) * (HALF // 16)]), gate_t[1][:, cols], MULT)
        for h in range(2):
            cols = slice(h * HALF, (h + 1) * HALF)
            nc.vector.tensor_tensor(result[:, cols], first[:, cols], second[:, cols], ADD)
            nc.sync.dma_start(out[:, cols], result[:, cols])
